import numpy as np
import ml_dtypes


def mxq(x, axis, fmt="e4m3"):
    dtype, down = {"e4m3": (ml_dtypes.float8_e4m3fn, 7), "e5m2": (ml_dtypes.float8_e5m2, 14)}[fmt]
    v = np.moveaxis(np.asarray(x, np.float32).astype(ml_dtypes.bfloat16).astype(np.float64), axis, -1)
    blocks = v.reshape(v.shape[:-1] + (-1, 32))
    amax = np.abs(blocks).max(-1, keepdims=True)
    byte = np.maximum(np.where(amax > 0, np.frexp(amax)[1] - 1 + 127, 0) - down, 1)
    scale = np.exp2(byte - 127.0)
    codes = (blocks / scale).astype(np.float32).astype(dtype).astype(np.float64)
    return np.moveaxis((codes * scale).reshape(v.shape), -1, axis)


WIDE = False


def mx_kscale(k):
    if not WIDE:
        return np.ones(k)
    levels = np.array([18, -18])
    if k % 512:
        return np.exp2(np.random.permutation(np.resize(levels, k // 32))).repeat(32)
    a = np.empty((k // 512, 16))
    for p in range(k // 512):
        a[p, :8] = np.random.permutation(np.resize(levels, 8))
        for g in range(8):
            far = levels[np.abs(levels - a[p, g]) >= 10]
            a[p, g + 8] = far[np.random.randint(len(far))]
    return np.exp2(a.ravel()).repeat(32)


def f64(x):
    return np.asarray(x).astype(np.float64)


def striped(idx):
    return np.tile(np.asarray(idx).reshape(-1, 16).T, (8, 1)).astype(np.uint16)


def unstriped(offs):
    return offs[:16].T.reshape(-1).astype(np.int64)


def setup_inputs():
    n = np.random.standard_normal
    uni = np.random.uniform
    idx = np.random.permutation(2048)[:512]
    f_d = mx_kscale(512)
    f_e = mx_kscale(512)
    f_i = np.ones(2048)
    f_i[idx] = mx_kscale(512)
    return {
        "aT": (n((512, 2048)) / np.sqrt(512) * f_d[:, None] * f_i[None, :]).astype(np.float32),
        "bT": (n((512, 2048)) * f_e[:, None] / f_i[None, :]).astype(np.float32),
        "tg": (n((512, 512))).astype(np.float32),
        "wm": (uni(0.75, 1.3, (512, 512))).astype(np.float32),
        "ca": (uni(0.75, 1.3, (512, 1)) / f_d[:, None]).astype(np.float32),
        "cb": np.tile(uni(0.75, 1.3, 512) / f_e, (128, 1)).astype(np.float32),
        "offs": striped(idx),
    }


def reference(aT, bT, tg, wm, ca, cb, offs):
    idx = unstriped(offs)
    aT_i = f64(aT)[:, idx]
    bT_i = f64(bT)[:, idx]
    C = mxq(aT_i, 1, "e4m3") @ mxq(bT_i, 1, "e4m3").T
    M = f64(wm) * f64(ca) * f64(cb)[:1] * (f64(ca) * f64(cb)[:1] * C - f64(tg))
    da = mxq(M, 1, "e5m2") @ mxq(bT_i, 0, "e4m3")
    out_0 = np.zeros((512, 2048))
    out_0[:, idx] = da
    db = mxq(M, 0, "e5m2").T @ mxq(aT_i, 0, "e4m3")
    out_1 = np.zeros((512, 2048))
    out_1[:, idx] = db
    return out_0, out_1

@@ -1,0 +1,291 @@
+from contextlib import ExitStack
+
+import concourse.mybir as mybir
+from concourse.masks import make_identity
+
+D, E, T, N = 512, 512, 2048, 512
+FLOPS = 3 * 2 * D * E * N
+
+F32 = mybir.dt.float32
+BF16 = mybir.dt.bfloat16
+U32 = mybir.dt.uint32
+U16 = mybir.dt.uint16
+U8 = mybir.dt.uint8
+E4M3 = mybir.dt.float8_e4m3fn_x4
+E5M2 = mybir.dt.float8_e5m2_x4
+COPY = mybir.ActivationFunctionType.Copy
+MULT = mybir.AluOpType.mult
+
+P = 128
+PACK = 4
+
+
+def tile_attend_gbarlow_ab_kernel(tc, aT, bT, tg, wm, ca, cb, offs, out_0, out_1):
+    nc = tc.nc
+    with ExitStack() as ctx:
+        keep = ctx.enter_context(tc.tile_pool(name="keep", bufs=1))
+        psum = ctx.enter_context(tc.psum_pool(name="psum", bufs=1))
+
+        def sb(name, width, dtype):
+            return keep.tile([P, width], dtype, name=name, align_bytes=64)
+
+        def planes(name, width, dtype):
+            return [sb(name + str(t), width, dtype) for t in range(PACK)]
+
+        def block(t, width=P):
+            return slice(t * width, (t + 1) * width)
+
+        def rows(x):
+            return x.rearrange("(p t) n -> t p n", t=PACK)
+
+        offsets = keep.tile([P, N // 16], U16, name="offsets")
+        ident = sb("ident", P, F32)
+        a_raw, b_raw = planes("a_raw", T, F32), planes("b_raw", T, F32)
+        wm_raw, tg_raw = planes("wm_raw", E, F32), planes("tg_raw", E, F32)
+        ca_col, cb_col = sb("ca_col", PACK, F32), sb("cb_col", PACK, F32)
+        cb_row = sb("cb_row", E, F32)
+        got = sb("got", 2 * PACK * N, BF16)
+        b_got, a_got = got[:, block(0, PACK * N)], got[:, block(1, PACK * N)]
+        spare = [tile[:] for tile in planes("spare", N, BF16)]
+        b_turn = [got[:, block(2, N)], got[:, block(3, N)], got[:, block(4, N)], spare[0]]
+        a_turn = [spare[1], spare[0], spare[1], spare[0]]
+        ca_first = got[:, block(5, N)].bitcast(F32)[:, 0:1]
+        a_i_codes, a_i_scales = planes("a_i_codes", P, U32), planes("a_i_scales", P, U8)
+        b_i_codes, b_i_scales = sb("b_i_codes", E, U32), sb("b_i_scales", E, U8)
+        a_weave, b_weave = sb("a_weave", PACK * N, BF16), sb("b_weave", PACK * N, BF16)
+        a_d_codes, a_d_scales = sb("a_d_codes", N, U32), sb("a_d_scales", N, U8)
+        b_e_codes, b_e_scales = sb("b_e_codes", N, U32), sb("b_e_scales", N, U8)
+        scaled = planes("scaled", E, F32)
+        ws_t = planes("ws_t", E, F32)
+        wa = [None] + ws_t[:-1]
+        m_e = [got[:, block(6, N)], got[:, block(7, N)], spare[2], spare[3]]
+        m_e_codes, m_e_scales = planes("m_e_codes", P, U32), planes("m_e_scales", P, U8)
+        m_d = [sb("m_d" + str(h), 2 * E, BF16) for h in range(2)]
+        m_d_codes = [sb("m_d_codes" + str(h), 2 * P, U32) for h in range(2)]
+        m_d_scales = [sb("m_d_scales" + str(h), 2 * P, U8) for h in range(2)]
+        da_whole, db_whole = planes("da", N, F32), planes("db", N, F32)
+        da = [[tile[:, block(half, N // 2)] for half in range(2)] for tile in da_whole]
+        db = [[tile[:, block(half, N // 2)] for half in range(2)] for tile in db_whole]
+        da[2] = [da[2][0], ws_t[3][:, block(0, N // 2)]]
+        windows = planes("window", T, F32)
+
+        turn_ps = psum.tile([P, 512], F32, name="turn_ps")
+        c_ps = psum.tile([P, 512], F32, name="c_ps")
+        wa_ps = psum.tile([P, 512], F32, name="wa_ps")
+        z_ps = psum.tile([P, 512], F32, name="z_ps")
+        grad_ps = [psum.tile([P, 512], F32, name="grad_ps" + str(h)) for h in range(2)]
+        back_ps = [psum.tile([P, 512], F32, name="back_ps" + str(h)) for h in range(2)]
+
+        a_rows, b_rows, wm_rows, tg_rows = rows(aT), rows(bT), rows(wm), rows(tg)
+        nc.sync.dma_start(out=b_raw[0][:], in_=b_rows[0])
+        nc.sync.dma_start(offsets[:], offs)
+        nc.sync.dma_start(out=cb_col[:], in_=cb[0:1, :].rearrange("o (q s) -> q (o s)", s=PACK))
+        nc.sync.dma_start(out=b_raw[1][:], in_=b_rows[1])
+        nc.sync.dma_start(out=ca_col[:], in_=ca.rearrange("(p t) o -> p (t o)", t=PACK))
+        nc.sync.dma_start(out=b_raw[2][:], in_=b_rows[2])
+        nc.sync.dma_start(out=b_raw[3][:], in_=b_rows[3])
+        nc.sync.dma_start(out=a_raw[0][:], in_=a_rows[0])
+
+        def load_weights(t):
+            nc.sync.dma_start(out=wm_raw[t][:], in_=wm_rows[t])
+            nc.sync.dma_start(out=tg_raw[t][:], in_=tg_rows[t])
+
+        load_weights(0)
+        nc.sync.dma_start(out=a_raw[1][:], in_=a_rows[1])
+        nc.sync.dma_start(out=a_raw[2][:], in_=a_rows[2])
+        load_weights(1)
+        nc.sync.dma_start(out=a_raw[3][:], in_=a_rows[3])
+        load_weights(2)
+        load_weights(3)
+
+        make_identity(nc, ident[:])
+
+        def quantize(codes, scales, values, fmt):
+            nc.vector.quantize_mx(out=codes.bitcast(fmt), scales=scales, in_=values)
+
+        def gather(got, raw, t):
+            nc.vector.tensor_copy(got[:, block(t, N)], raw[t][:].indirect(offsets[:]))
+
+        def turn(got, turned, t):
+            words = got[:, block(t, N)].bitcast(F32)
+            for u in range(2):
+                nc.tensor.transpose(turn_ps[:, block(u)], words[:, u : N // 2 : 2], ident[:])
+            nc.scalar.copy(
+                out=turned[t].bitcast(F32).rearrange("j (r u) -> j r u", u=2),
+                in_=turn_ps[:, 0 : 2 * P].rearrange("j (u r) -> j r u", u=2),
+            )
+
+        def weave(copy, woven, got, half):
+            cols = slice(half * (N // 8), (half + 1) * (N // 8))
+            copy(
+                out=woven[:].rearrange("p (c i t) -> p c t i", i=4, t=PACK)[:, cols],
+                in_=got.rearrange("p (t c i) -> p c t i", i=4, t=PACK)[:, cols],
+            )
+
+        def deal(out, raw, scale):
+            nc.scalar.activation(
+                out=out.rearrange("p (s c i) -> p c s i", s=PACK, i=4),
+                in_=raw.rearrange("p (c i s) -> p c s i", s=PACK, i=4),
+                func=COPY,
+                scale=scale,
+            )
+
+        def prepare_weights(t):
+            deal(wa[t][:], wm_raw[t][:], ca_col[:, t : t + 1])
+            for s in range(PACK):
+                nc.tensor.transpose(wa_ps[:, block(s)], wa[t][:, block(s)], ident[:])
+            deal(wa[t][:], tg_raw[t][:], -1.0)
+            for s in range(PACK):
+                nc.scalar.activation(
+                    out=ws_t[t][:, block(s)], in_=wa_ps[:, block(s)], func=COPY, scale=cb_col[:, s : s + 1]
+                )
+
+        def correlate(t):
+            quantize(a_i_codes[t][:], a_i_scales[t][:], a_turn[t], E4M3)
+            nc.tensor.matmul_mx(
+                out=c_ps[:],
+                lhsT=a_i_codes[t][:].bitcast(E4M3),
+                lhsT_scale=a_i_scales[t][:],
+                rhs=b_i_codes[:].bitcast(E4M3),
+                rhs_scale=b_i_scales[:],
+                start=True,
+                stop=True,
+            )
+
+        def scale_c(t):
+            nc.vector.scalar_tensor_tensor(
+                out=scaled[t][:], in0=c_ps[:], scalar=ca_first if t == 0 else ca_col[:, t : t + 1], in1=cb_row[:], op0=MULT, op1=MULT
+            )
+            for term, source in enumerate((wa[t], scaled[t])):
+                for s in range(PACK):
+                    nc.tensor.matmul(
+                        z_ps[:, block(s)],
+                        lhsT=source[:, block(s)],
+                        rhs=ident[:],
+                        is_transpose=True,
+                        start=(term == 0 and s == 0),
+                        stop=(term == 1 and s == PACK - 1),
+                    )
+
+        def form_m(t):
+            nc.vector.tensor_tensor(
+                out=m_e[t].rearrange("q (c i s) -> q c s i", s=PACK, i=4),
+                in0=z_ps[:].rearrange("q (s c i) -> q c s i", s=PACK, i=4),
+                in1=ws_t[t][:].rearrange("q (s c i) -> q c s i", s=PACK, i=4),
+                op=MULT,
+            )
+
+        def gradient(result, bank, codes, scales, moving_codes, moving_scales):
+            nc.tensor.matmul_mx(
+                out=bank[:],
+                lhsT=codes.bitcast(E5M2),
+                lhsT_scale=scales,
+                rhs=moving_codes[:].bitcast(E4M3),
+                rhs_scale=moving_scales[:],
+                start=True,
+                stop=True,
+            )
+            for half in range(2):
+                nc.scalar.copy(out=result[half], in_=bank[:, block(half, N // 2)])
+
+        def grad_a(t):
+            quantize(m_e_codes[t][:], m_e_scales[t][:], m_e[t], E5M2)
+            words = m_e[t].bitcast(F32)
+            for h in range(2):
+                nc.tensor.transpose(back_ps[h][:, block(t)], words[:, h : E // 2 : 2], ident[:])
+
+        def grad_a_product(t):
+            gradient(da[t], grad_ps[t % 2], m_e_codes[t][:], m_e_scales[t][:], b_e_codes, b_e_scales)
+
+        def scatter(window, values, half):
+            nc.vector.tensor_copy(
+                window[:].indirect(offsets[:, block(half, N // 32)]), values[half]
+            )
+
+        def scatter_whole(window, values):
+            nc.vector.tensor_copy(window[:].indirect(offsets[:]), values[:])
+
+        def store(out, t):
+            nc.sync.dma_start(out=rows(out)[t], in_=windows[t][:])
+
+        def turn_m_back(h):
+            nc.scalar.copy(
+                out=m_d[h][:].rearrange("p (j q t) -> p j q t", j=2, t=PACK),
+                in_=back_ps[h][:].bitcast(BF16).rearrange("p (t q j) -> p j q t", j=2, t=PACK),
+            )
+
+        def grad_b(h):
+            quantize(m_d_codes[h][:], m_d_scales[h][:], m_d[h][:], E5M2)
+            for j in range(2):
+                gradient(
+                    db[2 * h + j], grad_ps[j], m_d_codes[h][:, block(j)], m_d_scales[h][:, block(j)],
+                    a_d_codes, a_d_scales,
+                )
+
+        for s in range(PACK):
+            nc.tensor.transpose(z_ps[:, block(s)], cb_col[:, s : s + 1].to_broadcast([P, P]), ident[:])
+        nc.scalar.copy(out=cb_row[:], in_=z_ps[:])
+        nc.scalar.copy(out=ca_first, in_=ca_col[:, 0:1])
+
+        for s in range(PACK):
+            gather(b_got, b_raw, s)
+            turn(b_got, b_turn, s)
+            quantize(b_i_codes[:, block(s)], b_i_scales[:, block(s)], b_turn[s], E4M3)
+        weave(nc.scalar.copy, b_weave, b_got, 0)
+        weave(nc.vector.tensor_copy, b_weave, b_got, 1)
+        gather(a_got, a_raw, 0)
+        turn(a_got, a_turn, 0)
+        correlate(0)
+        wa[0] = keep.tile([P, E], F32, name="wa0", tag="a_raw0", align_bytes=64)
+        prepare_weights(0)
+        quantize(b_e_codes[:], b_e_scales[:], b_weave[:], E4M3)
+        scale_c(0)
+        gather(a_got, a_raw, 1)
+        turn(a_got, a_turn, 1)
+        form_m(0)
+        grad_a(0)
+        grad_a_product(0)
+        correlate(1)
+        gather(a_got, a_raw, 2)
+        turn(a_got, a_turn, 2)
+        prepare_weights(1)
+        scale_c(1)
+        correlate(2)
+        for t in range(PACK):
+            (nc.vector if t < 2 else nc.gpsimd).memset(windows[t][:].bitcast(mybir.dt.int32), 0)
+        scatter(windows[0], da[0], 0)
+        scatter(windows[0], da[0], 1)
+        store(out_0, 0)
+        form_m(1)
+        grad_a(1)
+        grad_a_product(1)
+        prepare_weights(2)
+        scale_c(2)
+        gather(a_got, a_raw, 3)
+        turn(a_got, a_turn, 3)
+        form_m(2)
+        grad_a(2)
+        correlate(3)
+        prepare_weights(3)
+        scatter_whole(windows[1], da_whole[1])
+        store(out_0, 1)
+        scale_c(3)
+        weave(nc.scalar.copy, a_weave, a_got, 0)
+        weave(nc.scalar.copy, a_weave, a_got, 1)
+        form_m(3)
+        grad_a_product(2)
+        scatter(windows[2], da[2], 0)
+        scatter(windows[2], da[2], 1)
+        store(out_0, 2)
+        grad_a(3)
+        turn_m_back(0)
+        grad_a_product(3)
+        turn_m_back(1)
+        quantize(a_d_codes[:], a_d_scales[:], a_weave[:], E4M3)
+        grad_b(0)
+        scatter_whole(windows[3], da_whole[3])
+        store(out_0, 3)
+        grad_b(1)
+        for s in range(PACK):
+            scatter_whole(windows[s], db_whole[s])
+            store(out_1, s)

@@ -8,6 +8,7 @@ FLOPS = 3 * 2 * D * E * N
 
 F32 = mybir.dt.float32
 BF16 = mybir.dt.bfloat16
+I32 = mybir.dt.int32
 U32 = mybir.dt.uint32
 U16 = mybir.dt.uint16
 U8 = mybir.dt.uint8
@@ -15,6 +16,7 @@ E4M3 = mybir.dt.float8_e4m3fn_x4
 E5M2 = mybir.dt.float8_e5m2_x4
 COPY = mybir.ActivationFunctionType.Copy
 MULT = mybir.AluOpType.mult
+SUBTRACT = mybir.AluOpType.subtract
 
 P = 128
 PACK = 4
@@ -26,8 +28,8 @@ def tile_attend_gbarlow_ab_kernel(tc, aT, bT, tg, wm, ca, cb, offs, out_0, out_1
         keep = ctx.enter_context(tc.tile_pool(name="keep", bufs=1))
         psum = ctx.enter_context(tc.psum_pool(name="psum", bufs=1))
 
-        def sb(name, width, dtype):
-            return keep.tile([P, width], dtype, name=name, align_bytes=64)
+        def sb(name, width, dtype, tag=None):
+            return keep.tile([P, width], dtype, name=name, tag=tag or name, align_bytes=64)
 
         def planes(name, width, dtype):
             return [sb(name + str(t), width, dtype) for t in range(PACK)]
@@ -46,37 +48,36 @@ def tile_attend_gbarlow_ab_kernel(tc, aT, bT, tg, wm, ca, cb, offs, out_0, out_1
         cb_row = sb("cb_row", E, F32)
         got = sb("got", 2 * PACK * N, BF16)
         b_got, a_got = got[:, block(0, PACK * N)], got[:, block(1, PACK * N)]
-        spare = [tile[:] for tile in planes("spare", N, BF16)]
-        b_turn = [got[:, block(2, N)], got[:, block(3, N)], got[:, block(4, N)], spare[0]]
-        a_turn = [spare[1], spare[0], spare[1], spare[0]]
-        ca_first = got[:, block(5, N)].bitcast(F32)[:, 0:1]
+        a_turn = {0: got[:, block(5, N)]}
+        b_turn = [got[:, block(2, N)], got[:, block(3, N)], got[:, block(4, N)], sb("b_turn3", N, BF16)[:]]
         a_i_codes, a_i_scales = planes("a_i_codes", P, U32), planes("a_i_scales", P, U8)
         b_i_codes, b_i_scales = sb("b_i_codes", E, U32), sb("b_i_scales", E, U8)
-        a_weave, b_weave = sb("a_weave", PACK * N, BF16), sb("b_weave", PACK * N, BF16)
+        b_weave = sb("b_weave", PACK * N, BF16)
         a_d_codes, a_d_scales = sb("a_d_codes", N, U32), sb("a_d_scales", N, U8)
         b_e_codes, b_e_scales = sb("b_e_codes", N, U32), sb("b_e_scales", N, U8)
-        scaled = planes("scaled", E, F32)
-        ws_t = planes("ws_t", E, F32)
-        wa = [None] + ws_t[:-1]
-        m_e = [got[:, block(6, N)], got[:, block(7, N)], spare[2], spare[3]]
+        weight = sb("weight", E, F32)
+        later_residual = sb("later_residual", E, F32)
+        staged = {0: sb("staged0", N, F32)[:], 3: sb("staged3", N, F32)[:]}
+        residual = [got[:, 6 * N : 8 * N].bitcast(F32)] + [later_residual[:]] * (PACK - 1)
+        m_rows = sb("m_rows", PACK * E, BF16)
+        m_e = [later_residual[:, 0 : E // 2].bitcast(BF16)] + [sb("m_e" + str(t), E, BF16)[:] for t in range(1, PACK)]
         m_e_codes, m_e_scales = planes("m_e_codes", P, U32), planes("m_e_scales", P, U8)
-        m_d = [sb("m_d" + str(h), 2 * E, BF16) for h in range(2)]
-        m_d_codes = [sb("m_d_codes" + str(h), 2 * P, U32) for h in range(2)]
-        m_d_scales = [sb("m_d_scales" + str(h), 2 * P, U8) for h in range(2)]
-        da_whole, db_whole = planes("da", N, F32), planes("db", N, F32)
-        da = [[tile[:, block(half, N // 2)] for half in range(2)] for tile in da_whole]
-        db = [[tile[:, block(half, N // 2)] for half in range(2)] for tile in db_whole]
-        da[2] = [da[2][0], ws_t[3][:, block(0, N // 2)]]
+        m_weave = sb("m_weave", PACK * E, BF16)
+        m_d_codes, m_d_scales = sb("m_d_codes", E, U32), sb("m_d_scales", E, U8)
+        db = [tile[:] for tile in planes("db", N, F32)]
         windows = planes("window", T, F32)
 
-        turn_ps = psum.tile([P, 512], F32, name="turn_ps")
-        c_ps = psum.tile([P, 512], F32, name="c_ps")
-        wa_ps = psum.tile([P, 512], F32, name="wa_ps")
-        z_ps = psum.tile([P, 512], F32, name="z_ps")
-        grad_ps = [psum.tile([P, 512], F32, name="grad_ps" + str(h)) for h in range(2)]
+        turn_ps = [psum.tile([P, 512], F32, name="turn_ps" + str(h)) for h in range(2)]
         back_ps = [psum.tile([P, 512], F32, name="back_ps" + str(h)) for h in range(2)]
+        c_ps = [psum.tile([P, 512], F32, name="c_ps" + str(h)) for h in range(2)]
+        grad_ps = [psum.tile([P, 512], F32, name="grad_ps" + str(h)) for h in range(2)]
 
         a_rows, b_rows, wm_rows, tg_rows = rows(aT), rows(bT), rows(wm), rows(tg)
+
+        def load_weights(t):
+            nc.sync.dma_start(out=wm_raw[t][:], in_=wm_rows[t])
+            nc.sync.dma_start(out=tg_raw[t][:], in_=tg_rows[t])
+
         nc.sync.dma_start(out=b_raw[0][:], in_=b_rows[0])
         nc.sync.dma_start(offsets[:], offs)
         nc.sync.dma_start(out=cb_col[:], in_=cb[0:1, :].rearrange("o (q s) -> q (o s)", s=PACK))
@@ -85,11 +86,6 @@ def tile_attend_gbarlow_ab_kernel(tc, aT, bT, tg, wm, ca, cb, offs, out_0, out_1
         nc.sync.dma_start(out=b_raw[2][:], in_=b_rows[2])
         nc.sync.dma_start(out=b_raw[3][:], in_=b_rows[3])
         nc.sync.dma_start(out=a_raw[0][:], in_=a_rows[0])
-
-        def load_weights(t):
-            nc.sync.dma_start(out=wm_raw[t][:], in_=wm_rows[t])
-            nc.sync.dma_start(out=tg_raw[t][:], in_=tg_rows[t])
-
         load_weights(0)
         nc.sync.dma_start(out=a_raw[1][:], in_=a_rows[1])
         nc.sync.dma_start(out=a_raw[2][:], in_=a_rows[2])
@@ -99,6 +95,8 @@ def tile_attend_gbarlow_ab_kernel(tc, aT, bT, tg, wm, ca, cb, offs, out_0, out_1
         load_weights(3)
 
         make_identity(nc, ident[:])
+        for t in range(PACK):
+            (nc.vector if t < 2 else nc.gpsimd).memset(windows[t][:].bitcast(I32), 0)
 
         def quantize(codes, scales, values, fmt):
             nc.vector.quantize_mx(out=codes.bitcast(fmt), scales=scales, in_=values)
@@ -106,44 +104,29 @@ def tile_attend_gbarlow_ab_kernel(tc, aT, bT, tg, wm, ca, cb, offs, out_0, out_1
         def gather(got, raw, t):
             nc.vector.tensor_copy(got[:, block(t, N)], raw[t][:].indirect(offsets[:]))
 
-        def turn(got, turned, t):
-            words = got[:, block(t, N)].bitcast(F32)
+        def turn(source, turned, bank):
+            words = source.bitcast(F32)
             for u in range(2):
-                nc.tensor.transpose(turn_ps[:, block(u)], words[:, u : N // 2 : 2], ident[:])
+                nc.tensor.transpose(bank[:, block(u)], words[:, u : 2 * P : 2], ident[:])
             nc.scalar.copy(
-                out=turned[t].bitcast(F32).rearrange("j (r u) -> j r u", u=2),
-                in_=turn_ps[:, 0 : 2 * P].rearrange("j (u r) -> j r u", u=2),
+                out=turned.bitcast(F32).rearrange("j (r u) -> j r u", u=2),
+                in_=bank[:, 0 : 2 * P].rearrange("j (u r) -> j r u", u=2),
             )
 
-        def weave(copy, woven, got, half):
+        def turn_a(t):
+            turn(a_got[:, block(t, N)], a_turn[t], grad_ps[0] if t == 2 else turn_ps[t % 2])
+
+        def weave(copy, woven, source, half):
             cols = slice(half * (N // 8), (half + 1) * (N // 8))
             copy(
                 out=woven[:].rearrange("p (c i t) -> p c t i", i=4, t=PACK)[:, cols],
-                in_=got.rearrange("p (t c i) -> p c t i", i=4, t=PACK)[:, cols],
+                in_=source.rearrange("p (t c i) -> p c t i", i=4, t=PACK)[:, cols],
             )
-
-        def deal(out, raw, scale):
-            nc.scalar.activation(
-                out=out.rearrange("p (s c i) -> p c s i", s=PACK, i=4),
-                in_=raw.rearrange("p (c i s) -> p c s i", s=PACK, i=4),
-                func=COPY,
-                scale=scale,
-            )
-
-        def prepare_weights(t):
-            deal(wa[t][:], wm_raw[t][:], ca_col[:, t : t + 1])
-            for s in range(PACK):
-                nc.tensor.transpose(wa_ps[:, block(s)], wa[t][:, block(s)], ident[:])
-            deal(wa[t][:], tg_raw[t][:], -1.0)
-            for s in range(PACK):
-                nc.scalar.activation(
-                    out=ws_t[t][:, block(s)], in_=wa_ps[:, block(s)], func=COPY, scale=cb_col[:, s : s + 1]
-                )
 
         def correlate(t):
             quantize(a_i_codes[t][:], a_i_scales[t][:], a_turn[t], E4M3)
             nc.tensor.matmul_mx(
-                out=c_ps[:],
+                out=c_ps[t % 2][:],
                 lhsT=a_i_codes[t][:].bitcast(E4M3),
                 lhsT_scale=a_i_scales[t][:],
                 rhs=b_i_codes[:].bitcast(E4M3),
@@ -152,28 +135,37 @@ def tile_attend_gbarlow_ab_kernel(tc, aT, bT, tg, wm, ca, cb, offs, out_0, out_1
                 stop=True,
             )
 
-        def scale_c(t):
+        def form_weight(t):
             nc.vector.scalar_tensor_tensor(
-                out=scaled[t][:], in0=c_ps[:], scalar=ca_first if t == 0 else ca_col[:, t : t + 1], in1=cb_row[:], op0=MULT, op1=MULT
+                out=weight[:], in0=wm_raw[t][:], scalar=ca_col[:, t : t + 1], in1=cb_row[:], op0=MULT, op1=MULT
             )
-            for term, source in enumerate((wa[t], scaled[t])):
-                for s in range(PACK):
-                    nc.tensor.matmul(
-                        z_ps[:, block(s)],
-                        lhsT=source[:, block(s)],
-                        rhs=ident[:],
-                        is_transpose=True,
-                        start=(term == 0 and s == 0),
-                        stop=(term == 1 and s == PACK - 1),
-                    )
 
         def form_m(t):
-            nc.vector.tensor_tensor(
-                out=m_e[t].rearrange("q (c i s) -> q c s i", s=PACK, i=4),
-                in0=z_ps[:].rearrange("q (s c i) -> q c s i", s=PACK, i=4),
-                in1=ws_t[t][:].rearrange("q (s c i) -> q c s i", s=PACK, i=4),
-                op=MULT,
-            )
+            halves = [block(half, E // 2) for half in range(2)]
+            c_by_e = c_ps[t % 2][:].rearrange("p (s q) -> p q s", s=PACK)
+            for half, cols in enumerate(halves):
+                nc.vector.scalar_tensor_tensor(
+                    out=residual[t][:, cols].rearrange("p (q s) -> p q s", s=PACK),
+                    in0=c_by_e[:, block(half, P // 2)],
+                    scalar=ca_col[:, t : t + 1],
+                    in1=cb_row[:, cols].rearrange("p (q s) -> p q s", s=PACK),
+                    op0=MULT,
+                    op1=MULT,
+                )
+            for cols in halves:
+                nc.vector.tensor_tensor(
+                    out=residual[t][:, cols], in0=residual[t][:, cols], in1=tg_raw[t][:, cols], op=SUBTRACT
+                )
+            for cols in halves:
+                nc.vector.tensor_tensor(
+                    out=m_rows[:, block(t, E)][:, cols], in0=residual[t][:, cols], in1=weight[:, cols], op=MULT
+                )
+            turn(m_rows[:, block(t, E)], m_e[t], back_ps[t % 2])
+            if t != 1:
+                after_tg = sb("after_tg" + str(t), N + N // 2, F32, tag="tg_raw" + str(t))
+                a_turn[t + 1] = after_tg[:, N : N + N // 2].bitcast(BF16)
+            if t >= 2:
+                staged[t - 1] = after_tg[:, 0:N]
 
         def gradient(result, bank, codes, scales, moving_codes, moving_scales):
             nc.tensor.matmul_mx(
@@ -185,107 +177,84 @@ def tile_attend_gbarlow_ab_kernel(tc, aT, bT, tg, wm, ca, cb, offs, out_0, out_1
                 start=True,
                 stop=True,
             )
-            for half in range(2):
-                nc.scalar.copy(out=result[half], in_=bank[:, block(half, N // 2)])
+            nc.scalar.copy(out=result, in_=bank[:])
+
+        def quantize_m_e(t):
+            quantize(m_e_codes[t][:], m_e_scales[t][:], m_e[t], E5M2)
 
         def grad_a(t):
-            quantize(m_e_codes[t][:], m_e_scales[t][:], m_e[t], E5M2)
-            words = m_e[t].bitcast(F32)
-            for h in range(2):
-                nc.tensor.transpose(back_ps[h][:, block(t)], words[:, h : E // 2 : 2], ident[:])
+            gradient(staged[t], grad_ps[t % 2], m_e_codes[t][:], m_e_scales[t][:], b_e_codes, b_e_scales)
 
-        def grad_a_product(t):
-            gradient(da[t], grad_ps[t % 2], m_e_codes[t][:], m_e_scales[t][:], b_e_codes, b_e_scales)
-
-        def scatter(window, values, half):
-            nc.vector.tensor_copy(
-                window[:].indirect(offsets[:, block(half, N // 32)]), values[half]
-            )
-
-        def scatter_whole(window, values):
-            nc.vector.tensor_copy(window[:].indirect(offsets[:]), values[:])
-
-        def store(out, t):
-            nc.sync.dma_start(out=rows(out)[t], in_=windows[t][:])
-
-        def turn_m_back(h):
-            nc.scalar.copy(
-                out=m_d[h][:].rearrange("p (j q t) -> p j q t", j=2, t=PACK),
-                in_=back_ps[h][:].bitcast(BF16).rearrange("p (t q j) -> p j q t", j=2, t=PACK),
-            )
-
-        def grad_b(h):
-            quantize(m_d_codes[h][:], m_d_scales[h][:], m_d[h][:], E5M2)
-            for j in range(2):
+        def grad_b(half):
+            cols = block(half, E // 2)
+            quantize(m_d_codes[:, cols], m_d_scales[:, cols], m_weave[:, block(half, 2 * E)], E5M2)
+            for j in range(2 * half, 2 * half + 2):
                 gradient(
-                    db[2 * h + j], grad_ps[j], m_d_codes[h][:, block(j)], m_d_scales[h][:, block(j)],
-                    a_d_codes, a_d_scales,
+                    db[j], grad_ps[j % 2], m_d_codes[:, block(j)], m_d_scales[:, block(j)], a_d_codes, a_d_scales
                 )
 
+        def scatter(out_rows, values, t):
+            nc.vector.tensor_copy(windows[t][:].indirect(offsets[:]), values[t])
+            nc.sync.dma_start(out=out_rows[t], in_=windows[t][:])
+
         for s in range(PACK):
-            nc.tensor.transpose(z_ps[:, block(s)], cb_col[:, s : s + 1].to_broadcast([P, P]), ident[:])
-        nc.scalar.copy(out=cb_row[:], in_=z_ps[:])
-        nc.scalar.copy(out=ca_first, in_=ca_col[:, 0:1])
+            nc.tensor.transpose(c_ps[1][:, block(s)], cb_col[:, s : s + 1].to_broadcast([P, P]), ident[:])
+        nc.scalar.copy(
+            out=cb_row[:].rearrange("p (q s) -> p q s", s=PACK),
+            in_=c_ps[1][:].rearrange("p (s q) -> p q s", s=PACK),
+        )
 
         for s in range(PACK):
             gather(b_got, b_raw, s)
-            turn(b_got, b_turn, s)
+            turn(b_got[:, block(s, N)], b_turn[s], turn_ps[s % 2])
             quantize(b_i_codes[:, block(s)], b_i_scales[:, block(s)], b_turn[s], E4M3)
         weave(nc.scalar.copy, b_weave, b_got, 0)
         weave(nc.vector.tensor_copy, b_weave, b_got, 1)
+
+        da_rows, db_rows = rows(out_0), out_1.rearrange("(j q) n -> j q n", q=P)
         gather(a_got, a_raw, 0)
-        turn(a_got, a_turn, 0)
+        turn_a(0)
         correlate(0)
-        wa[0] = keep.tile([P, E], F32, name="wa0", tag="a_raw0", align_bytes=64)
-        prepare_weights(0)
+        form_weight(0)
         quantize(b_e_codes[:], b_e_scales[:], b_weave[:], E4M3)
-        scale_c(0)
         gather(a_got, a_raw, 1)
-        turn(a_got, a_turn, 1)
         form_m(0)
+        quantize_m_e(0)
         grad_a(0)
-        grad_a_product(0)
-        correlate(1)
         gather(a_got, a_raw, 2)
-        turn(a_got, a_turn, 2)
-        prepare_weights(1)
-        scale_c(1)
-        correlate(2)
-        for t in range(PACK):
-            (nc.vector if t < 2 else nc.gpsimd).memset(windows[t][:].bitcast(mybir.dt.int32), 0)
-        scatter(windows[0], da[0], 0)
-        scatter(windows[0], da[0], 1)
-        store(out_0, 0)
+        turn_a(1)
+        correlate(1)
+        form_weight(1)
         form_m(1)
-        grad_a(1)
-        grad_a_product(1)
-        prepare_weights(2)
-        scale_c(2)
-        gather(a_got, a_raw, 3)
-        turn(a_got, a_turn, 3)
+        a_turn[2] = sb("a_turn2", N, BF16)[:]
+        turn_a(2)
+        correlate(2)
+        scatter(da_rows, staged, 0)
+        a_last = sb("a_last", T, BF16, tag="m_e_codes0")
+        nc.scalar.activation(out=a_last[:], in_=a_raw[3][:], func=COPY)
+        nc.scalar.activation(out=a_got[:, block(3, N)], in_=a_last[:].indirect(offsets[:]), func=COPY)
+        quantize_m_e(1)
+        form_weight(2)
         form_m(2)
-        grad_a(2)
+        turn_a(3)
+        grad_a(1)
         correlate(3)
-        prepare_weights(3)
-        scatter_whole(windows[1], da_whole[1])
-        store(out_0, 1)
-        scale_c(3)
+        form_weight(3)
+        quantize_m_e(2)
+        scatter(da_rows, staged, 1)
+        a_weave = sb("a_weave", PACK * N, BF16, tag="m_e2")
         weave(nc.scalar.copy, a_weave, a_got, 0)
         weave(nc.scalar.copy, a_weave, a_got, 1)
         form_m(3)
-        grad_a_product(2)
-        scatter(windows[2], da[2], 0)
-        scatter(windows[2], da[2], 1)
-        store(out_0, 2)
-        grad_a(3)
-        turn_m_back(0)
-        grad_a_product(3)
-        turn_m_back(1)
+        grad_a(2)
         quantize(a_d_codes[:], a_d_scales[:], a_weave[:], E4M3)
+        quantize_m_e(3)
+        grad_a(3)
+        weave(nc.scalar.copy, m_weave, m_rows[:], 0)
+        weave(nc.scalar.copy, m_weave, m_rows[:], 1)
+        scatter(da_rows, staged, 2)
         grad_b(0)
-        scatter_whole(windows[3], da_whole[3])
-        store(out_0, 3)
         grad_b(1)
-        for s in range(PACK):
-            scatter_whole(windows[s], db_whole[s])
-            store(out_1, s)
+        scatter(da_rows, staged, 3)
+        for j in range(PACK):
+            scatter(db_rows, db, j)

@@ -43,24 +43,29 @@ def tile_attend_gbarlow_ab_kernel(tc, aT, bT, tg, wm, ca, cb, offs, out_0, out_1
         offsets = keep.tile([P, N // 16], U16, name="offsets")
         ident = sb("ident", P, F32)
         a_raw, b_raw = planes("a_raw", T, F32), planes("b_raw", T, F32)
-        wm_raw, tg_raw = planes("wm_raw", E, F32), planes("tg_raw", E, F32)
+        wm_raw = planes("wm_raw", E, F32)
+        tg_wide = [sb("tg_raw" + str(t), E + N // 2, F32) for t in range(PACK)]
+        tg_raw = [tile[:, 0:E] for tile in tg_wide]
         ca_col, cb_col = sb("ca_col", PACK, F32), sb("cb_col", PACK, F32)
         cb_row = sb("cb_row", E, F32)
         got = sb("got", 2 * PACK * N, BF16)
         b_got, a_got = got[:, block(0, PACK * N)], got[:, block(1, PACK * N)]
-        a_turn = {0: got[:, block(5, N)]}
+        a_turn = {0: got[:, block(5, N)], 2: sb("a_turn2", N, BF16)[:]}
         b_turn = [got[:, block(2, N)], got[:, block(3, N)], got[:, block(4, N)], sb("b_turn3", N, BF16)[:]]
         a_i_codes, a_i_scales = planes("a_i_codes", P, U32), planes("a_i_scales", P, U8)
         b_i_codes, b_i_scales = sb("b_i_codes", E, U32), sb("b_i_scales", E, U8)
         b_weave = sb("b_weave", PACK * N, BF16)
-        a_d_codes, a_d_scales = sb("a_d_codes", N, U32), sb("a_d_scales", N, U8)
+        a_d_scales = sb("a_d_scales", N, U8)
         b_e_codes, b_e_scales = sb("b_e_codes", N, U32), sb("b_e_scales", N, U8)
-        weight = sb("weight", E, F32)
+        shared = sb("shared", N + E, F32)
+        first_weight = sb("first_weight", E, F32)[:]
+        weight = [first_weight, first_weight, shared[:, N : N + E], sb("last_weight", E, F32)[:]]
         later_residual = sb("later_residual", E, F32)
-        staged = {0: sb("staged0", N, F32)[:], 3: sb("staged3", N, F32)[:]}
+        staged = [shared[:, 0:N]] + [tile[:, E // 2 : E // 2 + N] for tile in tg_wide[2:]] + [sb("staged3", N, F32)[:]]
         residual = [got[:, 6 * N : 8 * N].bitcast(F32)] + [later_residual[:]] * (PACK - 1)
         m_rows = sb("m_rows", PACK * E, BF16)
-        m_e = [later_residual[:, 0 : E // 2].bitcast(BF16)] + [sb("m_e" + str(t), E, BF16)[:] for t in range(1, PACK)]
+        m_e = [later_residual[:, 0 : E // 2].bitcast(BF16), shared[:, N - E // 4 : N + E // 4].bitcast(BF16)]
+        m_e = m_e + [sb("m_e2", E, BF16)[:], sb("m_e3", E, BF16)[:]]
         m_e_codes, m_e_scales = planes("m_e_codes", P, U32), planes("m_e_scales", P, U8)
         m_weave = sb("m_weave", PACK * E, BF16)
         m_d_codes, m_d_scales = sb("m_d_codes", E, U32), sb("m_d_scales", E, U8)
@@ -76,13 +81,13 @@ def tile_attend_gbarlow_ab_kernel(tc, aT, bT, tg, wm, ca, cb, offs, out_0, out_1
 
         def load_weights(t):
             nc.sync.dma_start(out=wm_raw[t][:], in_=wm_rows[t])
-            nc.sync.dma_start(out=tg_raw[t][:], in_=tg_rows[t])
+            nc.sync.dma_start(out=tg_raw[t], in_=tg_rows[t])
 
         nc.sync.dma_start(out=b_raw[0][:], in_=b_rows[0])
         nc.sync.dma_start(offsets[:], offs)
-        nc.sync.dma_start(out=cb_col[:], in_=cb[0:1, :].rearrange("o (q s) -> q (o s)", s=PACK))
+        nc.scalar.dma_start(out=cb_col[:], in_=cb[0:1, :].rearrange("o (q s) -> q (o s)", s=PACK))
         nc.sync.dma_start(out=b_raw[1][:], in_=b_rows[1])
-        nc.sync.dma_start(out=ca_col[:], in_=ca.rearrange("(p t) o -> p (t o)", t=PACK))
+        nc.scalar.dma_start(out=ca_col[:], in_=ca.rearrange("(p t) o -> p (t o)", t=PACK))
         nc.sync.dma_start(out=b_raw[2][:], in_=b_rows[2])
         nc.sync.dma_start(out=b_raw[3][:], in_=b_rows[3])
         nc.sync.dma_start(out=a_raw[0][:], in_=a_rows[0])
@@ -114,7 +119,7 @@ def tile_attend_gbarlow_ab_kernel(tc, aT, bT, tg, wm, ca, cb, offs, out_0, out_1
             )
 
         def turn_a(t):
-            turn(a_got[:, block(t, N)], a_turn[t], grad_ps[0] if t == 2 else turn_ps[t % 2])
+            turn(a_got[:, block(t, N)], a_turn[t], (turn_ps[0], turn_ps[1], c_ps[1], c_ps[0])[t])
 
         def weave(copy, woven, source, half):
             cols = slice(half * (N // 8), (half + 1) * (N // 8))
@@ -137,7 +142,7 @@ def tile_attend_gbarlow_ab_kernel(tc, aT, bT, tg, wm, ca, cb, offs, out_0, out_1
 
         def form_weight(t):
             nc.vector.scalar_tensor_tensor(
-                out=weight[:], in0=wm_raw[t][:], scalar=ca_col[:, t : t + 1], in1=cb_row[:], op0=MULT, op1=MULT
+                out=weight[t], in0=wm_raw[t][:], scalar=ca_col[:, t : t + 1], in1=cb_row[:], op0=MULT, op1=MULT
             )
 
         def form_m(t):
@@ -158,16 +163,11 @@ def tile_attend_gbarlow_ab_kernel(tc, aT, bT, tg, wm, ca, cb, offs, out_0, out_1
                 )
             for cols in halves:
                 nc.vector.tensor_tensor(
-                    out=m_rows[:, block(t, E)][:, cols], in0=residual[t][:, cols], in1=weight[:, cols], op=MULT
+                    out=m_rows[:, block(t, E)][:, cols], in0=residual[t][:, cols], in1=weight[t][:, cols], op=MULT
                 )
             turn(m_rows[:, block(t, E)], m_e[t], back_ps[t % 2])
-            if t != 1:
-                after_tg = sb("after_tg" + str(t), N + N // 2, F32, tag="tg_raw" + str(t))
-                a_turn[t + 1] = after_tg[:, N : N + N // 2].bitcast(BF16)
-            if t >= 2:
-                staged[t - 1] = after_tg[:, 0:N]
 
-        def gradient(result, bank, codes, scales, moving_codes, moving_scales):
+        def gradient(bank, codes, scales, moving_codes, moving_scales):
             nc.tensor.matmul_mx(
                 out=bank[:],
                 lhsT=codes.bitcast(E5M2),
@@ -177,21 +177,28 @@ def tile_attend_gbarlow_ab_kernel(tc, aT, bT, tg, wm, ca, cb, offs, out_0, out_1
                 start=True,
                 stop=True,
             )
-            nc.scalar.copy(out=result, in_=bank[:])
 
         def quantize_m_e(t):
             quantize(m_e_codes[t][:], m_e_scales[t][:], m_e[t], E5M2)
 
         def grad_a(t):
-            gradient(staged[t], grad_ps[t % 2], m_e_codes[t][:], m_e_scales[t][:], b_e_codes, b_e_scales)
+            gradient(grad_ps[t % 2], m_e_codes[t][:], m_e_scales[t][:], b_e_codes, b_e_scales)
+
+        def stage_a(t, half):
+            cols = block(half, N // 2)
+            nc.scalar.copy(out=staged[t][:, cols], in_=grad_ps[t % 2][:, cols])
 
         def grad_b(half):
             cols = block(half, E // 2)
             quantize(m_d_codes[:, cols], m_d_scales[:, cols], m_weave[:, block(half, 2 * E)], E5M2)
             for j in range(2 * half, 2 * half + 2):
-                gradient(
-                    db[j], grad_ps[j % 2], m_d_codes[:, block(j)], m_d_scales[:, block(j)], a_d_codes, a_d_scales
-                )
+                gradient(grad_ps[j % 2], m_d_codes[:, block(j)], m_d_scales[:, block(j)], a_d_codes, a_d_scales)
+                nc.scalar.copy(out=db[j], in_=grad_ps[j % 2][:])
+
+        def scatter_half(values, t, half):
+            nc.vector.tensor_copy(
+                windows[t][:].indirect(offsets[:, block(half, N // 32)]), values[t][:, block(half, N // 2)]
+            )
 
         def scatter(out_rows, values, t):
             nc.vector.tensor_copy(windows[t][:].indirect(offsets[:]), values[t])
@@ -221,35 +228,47 @@ def tile_attend_gbarlow_ab_kernel(tc, aT, bT, tg, wm, ca, cb, offs, out_0, out_1
         form_m(0)
         quantize_m_e(0)
         grad_a(0)
+        stage_a(0, 0)
         gather(a_got, a_raw, 2)
+        a_turn[1] = sb("a_turn1", N, BF16, tag="tg_raw0")[:]
         turn_a(1)
         correlate(1)
         form_weight(1)
         form_m(1)
-        a_turn[2] = sb("a_turn2", N, BF16)[:]
+        scatter_half(staged, 0, 0)
         turn_a(2)
         correlate(2)
-        scatter(da_rows, staged, 0)
-        a_last = sb("a_last", T, BF16, tag="m_e_codes0")
+        quantize_m_e(1)
+        stage_a(0, 1)
+        grad_a(1)
+        stage_a(1, 1)
+        form_weight(2)
+        scatter_half(staged, 0, 1)
+        nc.sync.dma_start(out=da_rows[0], in_=windows[0][:])
+        form_m(2)
+        stage_a(1, 0)
+        a_last = sb("a_last", T, BF16, tag="m_e_codes1")
         nc.scalar.activation(out=a_last[:], in_=a_raw[3][:], func=COPY)
         nc.scalar.activation(out=a_got[:, block(3, N)], in_=a_last[:].indirect(offsets[:]), func=COPY)
-        quantize_m_e(1)
-        form_weight(2)
-        form_m(2)
-        turn_a(3)
-        grad_a(1)
-        correlate(3)
-        form_weight(3)
-        quantize_m_e(2)
         scatter(da_rows, staged, 1)
+        a_turn[3] = weight[3][:, 0 : N // 2].bitcast(BF16)
+        turn_a(3)
+        correlate(3)
+        quantize_m_e(2)
+        grad_a(2)
+        stage_a(2, 1)
+        form_weight(3)
         a_weave = sb("a_weave", PACK * N, BF16, tag="m_e2")
         weave(nc.scalar.copy, a_weave, a_got, 0)
         weave(nc.scalar.copy, a_weave, a_got, 1)
         form_m(3)
-        grad_a(2)
-        quantize(a_d_codes[:], a_d_scales[:], a_weave[:], E4M3)
+        stage_a(2, 0)
         quantize_m_e(3)
         grad_a(3)
+        stage_a(3, 0)
+        stage_a(3, 1)
+        a_d_codes = sb("a_d_codes", N, U32, tag="m_e3")
+        quantize(a_d_codes[:], a_d_scales[:], a_weave[:], E4M3)
         weave(nc.scalar.copy, m_weave, m_rows[:], 0)
         weave(nc.scalar.copy, m_weave, m_rows[:], 1)
         scatter(da_rows, staged, 2)

@@ -55,13 +55,14 @@ def tile_attend_gbarlow_ab_kernel(tc, aT, bT, tg, wm, ca, cb, offs, out_0, out_1
         a_i_codes, a_i_scales = planes("a_i_codes", P, U32), planes("a_i_scales", P, U8)
         b_i_codes, b_i_scales = sb("b_i_codes", E, U32), sb("b_i_scales", E, U8)
         b_weave = sb("b_weave", PACK * N, BF16)
-        a_d_scales = sb("a_d_scales", N, U8)
+        a_d_codes, a_d_scales = sb("a_d_codes", N, U32), sb("a_d_scales", N, U8)
         b_e_codes, b_e_scales = sb("b_e_codes", N, U32), sb("b_e_scales", N, U8)
         shared = sb("shared", N + E, F32)
         first_weight = sb("first_weight", E, F32)[:]
-        weight = [first_weight, first_weight, shared[:, N : N + E], sb("last_weight", E, F32)[:]]
+        weight = [first_weight, first_weight, shared[:, N : N + E], sb("weight3", E, F32)[:]]
         later_residual = sb("later_residual", E, F32)
         staged = [shared[:, 0:N]] + [tile[:, E // 2 : E // 2 + N] for tile in tg_wide[2:]] + [sb("staged3", N, F32)[:]]
+        halves_of = [[whole[:, block(half, N // 2)] for half in range(2)] for whole in staged]
         residual = [got[:, 6 * N : 8 * N].bitcast(F32)] + [later_residual[:]] * (PACK - 1)
         m_rows = sb("m_rows", PACK * E, BF16)
         m_e = [later_residual[:, 0 : E // 2].bitcast(BF16), shared[:, N - E // 4 : N + E // 4].bitcast(BF16)]
@@ -165,7 +166,9 @@ def tile_attend_gbarlow_ab_kernel(tc, aT, bT, tg, wm, ca, cb, offs, out_0, out_1
                 nc.vector.tensor_tensor(
                     out=m_rows[:, block(t, E)][:, cols], in0=residual[t][:, cols], in1=weight[t][:, cols], op=MULT
                 )
-            turn(m_rows[:, block(t, E)], m_e[t], back_ps[t % 2])
+
+        def turn_m(t):
+            turn(m_rows[:, block(t, E)], m_e[t], grad_ps[0] if t == 3 else back_ps[t % 2])
 
         def gradient(bank, codes, scales, moving_codes, moving_scales):
             nc.tensor.matmul_mx(
@@ -185,8 +188,7 @@ def tile_attend_gbarlow_ab_kernel(tc, aT, bT, tg, wm, ca, cb, offs, out_0, out_1
             gradient(grad_ps[t % 2], m_e_codes[t][:], m_e_scales[t][:], b_e_codes, b_e_scales)
 
         def stage_a(t, half):
-            cols = block(half, N // 2)
-            nc.scalar.copy(out=staged[t][:, cols], in_=grad_ps[t % 2][:, cols])
+            nc.scalar.copy(out=halves_of[t][half], in_=grad_ps[t % 2][:, block(half, N // 2)])
 
         def grad_b(half):
             cols = block(half, E // 2)
@@ -195,9 +197,9 @@ def tile_attend_gbarlow_ab_kernel(tc, aT, bT, tg, wm, ca, cb, offs, out_0, out_1
                 gradient(grad_ps[j % 2], m_d_codes[:, block(j)], m_d_scales[:, block(j)], a_d_codes, a_d_scales)
                 nc.scalar.copy(out=db[j], in_=grad_ps[j % 2][:])
 
-        def scatter_half(values, t, half):
+        def scatter_half(t, half):
             nc.vector.tensor_copy(
-                windows[t][:].indirect(offsets[:, block(half, N // 32)]), values[t][:, block(half, N // 2)]
+                windows[t][:].indirect(offsets[:, block(half, N // 32)]), halves_of[t][half]
             )
 
         def scatter(out_rows, values, t):
@@ -226,6 +228,7 @@ def tile_attend_gbarlow_ab_kernel(tc, aT, bT, tg, wm, ca, cb, offs, out_0, out_1
         quantize(b_e_codes[:], b_e_scales[:], b_weave[:], E4M3)
         gather(a_got, a_raw, 1)
         form_m(0)
+        turn_m(0)
         quantize_m_e(0)
         grad_a(0)
         stage_a(0, 0)
@@ -235,7 +238,8 @@ def tile_attend_gbarlow_ab_kernel(tc, aT, bT, tg, wm, ca, cb, offs, out_0, out_1
         correlate(1)
         form_weight(1)
         form_m(1)
-        scatter_half(staged, 0, 0)
+        turn_m(1)
+        scatter_half(0, 0)
         turn_a(2)
         correlate(2)
         quantize_m_e(1)
@@ -243,9 +247,10 @@ def tile_attend_gbarlow_ab_kernel(tc, aT, bT, tg, wm, ca, cb, offs, out_0, out_1
         grad_a(1)
         stage_a(1, 1)
         form_weight(2)
-        scatter_half(staged, 0, 1)
+        scatter_half(0, 1)
         nc.sync.dma_start(out=da_rows[0], in_=windows[0][:])
         form_m(2)
+        turn_m(2)
         stage_a(1, 0)
         a_last = sb("a_last", T, BF16, tag="m_e_codes1")
         nc.scalar.activation(out=a_last[:], in_=a_raw[3][:], func=COPY)
@@ -256,22 +261,24 @@ def tile_attend_gbarlow_ab_kernel(tc, aT, bT, tg, wm, ca, cb, offs, out_0, out_1
         correlate(3)
         quantize_m_e(2)
         grad_a(2)
-        stage_a(2, 1)
         form_weight(3)
         a_weave = sb("a_weave", PACK * N, BF16, tag="m_e2")
         weave(nc.scalar.copy, a_weave, a_got, 0)
         weave(nc.scalar.copy, a_weave, a_got, 1)
         form_m(3)
         stage_a(2, 0)
+        turn_m(3)
+        stage_a(2, 1)
+        quantize(a_d_codes[:], a_d_scales[:], a_weave[:], E4M3)
+        scatter_half(2, 0)
         quantize_m_e(3)
         grad_a(3)
         stage_a(3, 0)
         stage_a(3, 1)
-        a_d_codes = sb("a_d_codes", N, U32, tag="m_e3")
-        quantize(a_d_codes[:], a_d_scales[:], a_weave[:], E4M3)
         weave(nc.scalar.copy, m_weave, m_rows[:], 0)
         weave(nc.scalar.copy, m_weave, m_rows[:], 1)
-        scatter(da_rows, staged, 2)
+        scatter_half(2, 1)
+        nc.sync.dma_start(out=da_rows[2], in_=windows[2][:])
         grad_b(0)
         grad_b(1)
         scatter(da_rows, staged, 3)

@@ -44,61 +44,61 @@ def tile_attend_gbarlow_ab_kernel(tc, aT, bT, tg, wm, ca, cb, offs, out_0, out_1
         ident = sb("ident", P, F32)
         a_raw, b_raw = planes("a_raw", T, F32), planes("b_raw", T, F32)
         wm_raw = planes("wm_raw", E, F32)
-        tg_wide = [sb("tg_raw" + str(t), E + N // 2, F32) for t in range(PACK)]
-        tg_raw = [tile[:, 0:E] for tile in tg_wide]
         ca_col, cb_col = sb("ca_col", PACK, F32), sb("cb_col", PACK, F32)
-        cb_row = sb("cb_row", E, F32)
-        got = sb("got", 2 * PACK * N, BF16)
+        cb_row, scale2 = sb("cb_row", E, F32), sb("scale2", E, F32)
+        got = sb("got", 8 * N, BF16)
         b_got, a_got = got[:, block(0, PACK * N)], got[:, block(1, PACK * N)]
-        a_turn = {0: got[:, block(5, N)], 2: sb("a_turn2", N, BF16)[:]}
-        b_turn = [got[:, block(2, N)], got[:, block(3, N)], got[:, block(4, N)], sb("b_turn3", N, BF16)[:]]
+        tg_raw = [tile[:] for tile in planes("tg_raw", E, F32)]
+        a_turn = [got[:, block(5, N)]] + [sb("a_turn" + str(t), N, BF16)[:] for t in range(1, PACK)]
+        b_turn = {0: got[:, block(2, N)], 1: got[:, block(3, N)], 2: got[:, block(4, N)]}
         a_i_codes, a_i_scales = planes("a_i_codes", P, U32), planes("a_i_scales", P, U8)
         b_i_codes, b_i_scales = sb("b_i_codes", E, U32), sb("b_i_scales", E, U8)
         b_weave = sb("b_weave", PACK * N, BF16)
         a_d_codes, a_d_scales = sb("a_d_codes", N, U32), sb("a_d_scales", N, U8)
-        b_e_codes, b_e_scales = sb("b_e_codes", N, U32), sb("b_e_scales", N, U8)
-        shared = sb("shared", N + E, F32)
-        first_weight = sb("first_weight", E, F32)[:]
-        weight = [first_weight, first_weight, shared[:, N : N + E], sb("weight3", E, F32)[:]]
-        later_residual = sb("later_residual", E, F32)
-        staged = [shared[:, 0:N]] + [tile[:, E // 2 : E // 2 + N] for tile in tg_wide[2:]] + [sb("staged3", N, F32)[:]]
-        halves_of = [[whole[:, block(half, N // 2)] for half in range(2)] for whole in staged]
-        residual = [got[:, 6 * N : 8 * N].bitcast(F32)] + [later_residual[:]] * (PACK - 1)
+        b_e_scales = sb("b_e_scales", N, U8)
+        weight = {}
+        residual = {t: sb("residual" + str(t), E, F32)[:] for t in range(1, PACK)}
         m_rows = sb("m_rows", PACK * E, BF16)
-        m_e = [later_residual[:, 0 : E // 2].bitcast(BF16), shared[:, N - E // 4 : N + E // 4].bitcast(BF16)]
-        m_e = m_e + [sb("m_e2", E, BF16)[:], sb("m_e3", E, BF16)[:]]
-        m_e_codes, m_e_scales = planes("m_e_codes", P, U32), planes("m_e_scales", P, U8)
+        second = sb("second", N // 2, F32)
+        m_e = [sb("m_e0", E, BF16)[:], got[:, block(7, N)], sb("m_e2", E, BF16)[:], second[:].bitcast(BF16)]
+        staged = {3: m_rows[:, 0 : 2 * N].bitcast(F32)}
+        staged_half = {1: [sb("staged1" + h, N // 2, F32)[:] for h in "ab"], 2: [tg_raw[3][:, 0 : N // 2], second[:]]}
+        m_e_codes = {t: sb("m_e_codes" + str(t), P, U32) for t in range(1, PACK)}
+        m_e_scales = planes("m_e_scales", P, U8)
         m_weave = sb("m_weave", PACK * E, BF16)
         m_d_codes, m_d_scales = sb("m_d_codes", E, U32), sb("m_d_scales", E, U8)
         db = [tile[:] for tile in planes("db", N, F32)]
         windows = planes("window", T, F32)
 
         turn_ps = [psum.tile([P, 512], F32, name="turn_ps" + str(h)) for h in range(2)]
-        back_ps = [psum.tile([P, 512], F32, name="back_ps" + str(h)) for h in range(2)]
-        c_ps = [psum.tile([P, 512], F32, name="c_ps" + str(h)) for h in range(2)]
+        c_ps = [psum.tile([P, 512], F32, name="c_ps" + str(h)) for h in range(3)]
+        cb_ps = psum.tile([P, 512], F32, name="cb_ps")
+        c_bank = (c_ps[0], c_ps[1], c_ps[2], c_ps[0])
         grad_ps = [psum.tile([P, 512], F32, name="grad_ps" + str(h)) for h in range(2)]
 
         a_rows, b_rows, wm_rows, tg_rows = rows(aT), rows(bT), rows(wm), rows(tg)
 
-        def load_weights(t):
-            nc.sync.dma_start(out=wm_raw[t][:], in_=wm_rows[t])
-            nc.sync.dma_start(out=tg_raw[t], in_=tg_rows[t])
+        def load(tile, source):
+            nc.sync.dma_start(out=tile, in_=source)
 
-        nc.sync.dma_start(out=b_raw[0][:], in_=b_rows[0])
+        load(b_raw[0][:], b_rows[0])
         nc.sync.dma_start(offsets[:], offs)
         nc.scalar.dma_start(out=cb_col[:], in_=cb[0:1, :].rearrange("o (q s) -> q (o s)", s=PACK))
-        nc.sync.dma_start(out=b_raw[1][:], in_=b_rows[1])
+        load(b_raw[1][:], b_rows[1])
         nc.scalar.dma_start(out=ca_col[:], in_=ca.rearrange("(p t) o -> p (t o)", t=PACK))
-        nc.sync.dma_start(out=b_raw[2][:], in_=b_rows[2])
-        nc.sync.dma_start(out=b_raw[3][:], in_=b_rows[3])
-        nc.sync.dma_start(out=a_raw[0][:], in_=a_rows[0])
-        load_weights(0)
-        nc.sync.dma_start(out=a_raw[1][:], in_=a_rows[1])
-        nc.sync.dma_start(out=a_raw[2][:], in_=a_rows[2])
-        load_weights(1)
-        nc.sync.dma_start(out=a_raw[3][:], in_=a_rows[3])
-        load_weights(2)
-        load_weights(3)
+        load(b_raw[2][:], b_rows[2])
+        load(b_raw[3][:], b_rows[3])
+        load(a_raw[0][:], a_rows[0])
+        load(wm_raw[0][:], wm_rows[0])
+        load(a_raw[1][:], a_rows[1])
+        load(tg_raw[0], tg_rows[0])
+        load(a_raw[2][:], a_rows[2])
+        load(wm_raw[1][:], wm_rows[1])
+        load(tg_raw[1], tg_rows[1])
+        load(a_raw[3][:], a_rows[3])
+        for t in range(2, PACK):
+            load(wm_raw[t][:], wm_rows[t])
+            load(tg_raw[t], tg_rows[t])
 
         make_identity(nc, ident[:])
         for t in range(PACK):
@@ -107,8 +107,8 @@ def tile_attend_gbarlow_ab_kernel(tc, aT, bT, tg, wm, ca, cb, offs, out_0, out_1
         def quantize(codes, scales, values, fmt):
             nc.vector.quantize_mx(out=codes.bitcast(fmt), scales=scales, in_=values)
 
-        def gather(got, raw, t):
-            nc.vector.tensor_copy(got[:, block(t, N)], raw[t][:].indirect(offsets[:]))
+        def gather(target, raw, t):
+            nc.vector.tensor_copy(target[:, block(t, N)], raw[t][:].indirect(offsets[:]))
 
         def turn(source, turned, bank):
             words = source.bitcast(F32)
@@ -120,10 +120,10 @@ def tile_attend_gbarlow_ab_kernel(tc, aT, bT, tg, wm, ca, cb, offs, out_0, out_1
             )
 
         def turn_a(t):
-            turn(a_got[:, block(t, N)], a_turn[t], (turn_ps[0], turn_ps[1], c_ps[1], c_ps[0])[t])
+            turn(a_got[:, block(t, N)], a_turn[t], turn_ps[t % 2])
 
-        def weave(copy, woven, source, half):
-            cols = slice(half * (N // 8), (half + 1) * (N // 8))
+        def weave(copy, woven, source, part, parts):
+            cols = block(part, N // PACK // parts)
             copy(
                 out=woven[:].rearrange("p (c i t) -> p c t i", i=4, t=PACK)[:, cols],
                 in_=source.rearrange("p (t c i) -> p c t i", i=4, t=PACK)[:, cols],
@@ -132,7 +132,7 @@ def tile_attend_gbarlow_ab_kernel(tc, aT, bT, tg, wm, ca, cb, offs, out_0, out_1
         def correlate(t):
             quantize(a_i_codes[t][:], a_i_scales[t][:], a_turn[t], E4M3)
             nc.tensor.matmul_mx(
-                out=c_ps[t % 2][:],
+                out=c_bank[t][:],
                 lhsT=a_i_codes[t][:].bitcast(E4M3),
                 lhsT_scale=a_i_scales[t][:],
                 rhs=b_i_codes[:].bitcast(E4M3),
@@ -141,34 +141,47 @@ def tile_attend_gbarlow_ab_kernel(tc, aT, bT, tg, wm, ca, cb, offs, out_0, out_1
                 stop=True,
             )
 
+        def by_e(bank):
+            return bank[:].rearrange("p (s q) -> p q s", s=PACK)
+
+        def in_fours(x):
+            return x.rearrange("p (q s) -> p q s", s=PACK)
+
         def form_weight(t):
             nc.vector.scalar_tensor_tensor(
-                out=weight[t], in0=wm_raw[t][:], scalar=ca_col[:, t : t + 1], in1=cb_row[:], op0=MULT, op1=MULT
+                out=in_fours(weight[t]),
+                in0=in_fours(wm_raw[t][:]),
+                scalar=ca_col[:, t : t + 1],
+                in1=by_e(cb_ps),
+                op0=MULT,
+                op1=MULT,
             )
 
-        def form_m(t):
-            halves = [block(half, E // 2) for half in range(2)]
-            c_by_e = c_ps[t % 2][:].rearrange("p (s q) -> p q s", s=PACK)
-            for half, cols in enumerate(halves):
+        def scale_c(t, parts):
+            for part in range(parts):
+                cols = block(part, E // parts)
                 nc.vector.scalar_tensor_tensor(
-                    out=residual[t][:, cols].rearrange("p (q s) -> p q s", s=PACK),
-                    in0=c_by_e[:, block(half, P // 2)],
+                    out=in_fours(residual[t][:, cols]),
+                    in0=by_e(c_bank[t])[:, block(part, P // parts)],
                     scalar=ca_col[:, t : t + 1],
-                    in1=cb_row[:, cols].rearrange("p (q s) -> p q s", s=PACK),
+                    in1=in_fours(cb_row[:, cols]),
                     op0=MULT,
                     op1=MULT,
                 )
-            for cols in halves:
-                nc.vector.tensor_tensor(
+
+        def finish_m(t, engine, parts):
+            pieces = [block(part, E // parts) for part in range(parts)]
+            for cols in pieces:
+                engine.tensor_tensor(
                     out=residual[t][:, cols], in0=residual[t][:, cols], in1=tg_raw[t][:, cols], op=SUBTRACT
                 )
-            for cols in halves:
-                nc.vector.tensor_tensor(
+            for cols in pieces:
+                engine.tensor_tensor(
                     out=m_rows[:, block(t, E)][:, cols], in0=residual[t][:, cols], in1=weight[t][:, cols], op=MULT
                 )
 
         def turn_m(t):
-            turn(m_rows[:, block(t, E)], m_e[t], grad_ps[0] if t == 3 else back_ps[t % 2])
+            turn(m_rows[:, block(t, E)], m_e[t], (c_ps[1], c_ps[0], c_ps[0], c_ps[1])[t])
 
         def gradient(bank, codes, scales, moving_codes, moving_scales):
             nc.tensor.matmul_mx(
@@ -181,104 +194,111 @@ def tile_attend_gbarlow_ab_kernel(tc, aT, bT, tg, wm, ca, cb, offs, out_0, out_1
                 stop=True,
             )
 
-        def quantize_m_e(t):
-            quantize(m_e_codes[t][:], m_e_scales[t][:], m_e[t], E5M2)
-
         def grad_a(t):
+            quantize(m_e_codes[t][:], m_e_scales[t][:], m_e[t], E5M2)
             gradient(grad_ps[t % 2], m_e_codes[t][:], m_e_scales[t][:], b_e_codes, b_e_scales)
 
-        def stage_a(t, half):
-            nc.scalar.copy(out=halves_of[t][half], in_=grad_ps[t % 2][:, block(half, N // 2)])
+        def stage_a(t):
+            nc.scalar.copy(out=staged[t], in_=grad_ps[t % 2][:])
 
         def grad_b(half):
             cols = block(half, E // 2)
             quantize(m_d_codes[:, cols], m_d_scales[:, cols], m_weave[:, block(half, 2 * E)], E5M2)
             for j in range(2 * half, 2 * half + 2):
-                gradient(grad_ps[j % 2], m_d_codes[:, block(j)], m_d_scales[:, block(j)], a_d_codes, a_d_scales)
-                nc.scalar.copy(out=db[j], in_=grad_ps[j % 2][:])
+                bank = (c_ps[2], turn_ps[0], turn_ps[1], c_ps[0])[j]
+                gradient(bank, m_d_codes[:, block(j)], m_d_scales[:, block(j)], a_d_codes, a_d_scales)
+                nc.scalar.copy(out=db[j], in_=bank[:])
+
+        def stage_half(t, half):
+            nc.scalar.copy(out=staged_half[t][half], in_=grad_ps[t % 2][:, block(half, N // 2)])
 
         def scatter_half(t, half):
-            nc.vector.tensor_copy(
-                windows[t][:].indirect(offsets[:, block(half, N // 32)]), halves_of[t][half]
-            )
+            nc.vector.tensor_copy(windows[t][:].indirect(offsets[:, block(half, N // 32)]), staged_half[t][half])
+            if half == 1:
+                nc.sync.dma_start(out=da_rows[t], in_=windows[t][:])
 
         def scatter(out_rows, values, t):
             nc.vector.tensor_copy(windows[t][:].indirect(offsets[:]), values[t])
             nc.sync.dma_start(out=out_rows[t], in_=windows[t][:])
 
         for s in range(PACK):
-            nc.tensor.transpose(c_ps[1][:, block(s)], cb_col[:, s : s + 1].to_broadcast([P, P]), ident[:])
-        nc.scalar.copy(
-            out=cb_row[:].rearrange("p (q s) -> p q s", s=PACK),
-            in_=c_ps[1][:].rearrange("p (s q) -> p q s", s=PACK),
-        )
+            nc.tensor.transpose(cb_ps[:, block(s)], cb_col[:, s : s + 1].to_broadcast([P, P]), ident[:])
+        nc.scalar.copy(out=in_fours(cb_row[:]), in_=by_e(cb_ps))
+        nc.scalar.activation(out=scale2[:], in_=cb_row[:], func=COPY, scale=ca_col[:, 2:3])
+
+        def turn_b(s):
+            turn(b_got[:, block(s, N)], b_turn[s], turn_ps[(s + 1) % 2])
+            quantize(b_i_codes[:, block(s)], b_i_scales[:, block(s)], b_turn[s], E4M3)
 
         for s in range(PACK):
             gather(b_got, b_raw, s)
-            turn(b_got[:, block(s, N)], b_turn[s], turn_ps[s % 2])
-            quantize(b_i_codes[:, block(s)], b_i_scales[:, block(s)], b_turn[s], E4M3)
-        weave(nc.scalar.copy, b_weave, b_got, 0)
-        weave(nc.vector.tensor_copy, b_weave, b_got, 1)
+            if s < PACK - 1:
+                turn_b(s)
+        weave(nc.vector.tensor_copy, b_weave, b_got, 3, 4)
+        for part in range(3):
+            weave(nc.scalar.copy, b_weave, b_got, part, 4)
 
         da_rows, db_rows = rows(out_0), out_1.rearrange("(j q) n -> j q n", q=P)
         gather(a_got, a_raw, 0)
+        after_a0 = sb("after_a0", E + N // 2, F32, tag="a_raw0")
+        weight[0], b_turn[3] = after_a0[:, 0:E], after_a0[:, E : E + N // 2].bitcast(BF16)
+        form_weight(0)
+        turn_b(3)
+        b_e_codes = sb("b_e_codes", N, U32, tag="wm_raw0")
+        quantize(b_e_codes[:], b_e_scales[:], b_weave[:], E4M3)
         turn_a(0)
         correlate(0)
-        form_weight(0)
-        quantize(b_e_codes[:], b_e_scales[:], b_weave[:], E4M3)
         gather(a_got, a_raw, 1)
-        form_m(0)
-        turn_m(0)
-        quantize_m_e(0)
-        grad_a(0)
-        stage_a(0, 0)
-        gather(a_got, a_raw, 2)
-        a_turn[1] = sb("a_turn1", N, BF16, tag="tg_raw0")[:]
+        residual[0] = sb("residual0", E, F32, tag="a_raw1")[:]
+        scale_c(0, 2)
         turn_a(1)
+        finish_m(0, nc.vector, 2)
+        turn_m(0)
         correlate(1)
-        form_weight(1)
-        form_m(1)
-        turn_m(1)
-        scatter_half(0, 0)
+        gather(a_got, a_raw, 2)
+        m_e_codes[0] = sb("m_e_codes0", P, U32, tag="a_raw2")
+        grad_a(0)
         turn_a(2)
+        weight[1] = sb("weight1", E, F32, tag="m_e0")[:]
+        form_weight(1)
+        scale_c(1, 1)
+        staged[0] = sb("staged0", N, F32, tag="wm_raw1")[:]
+        stage_a(0)
         correlate(2)
-        quantize_m_e(1)
-        stage_a(0, 1)
+        finish_m(1, nc.gpsimd, 1)
+        weight[2] = sb("weight2", E, F32)[:]
+        nc.gpsimd.tensor_tensor(out=weight[2], in0=wm_raw[2][:], in1=scale2[:], op=MULT)
+        scatter(da_rows, staged, 0)
+        scale_c(2, 1)
+        turn_m(1)
         grad_a(1)
-        stage_a(1, 1)
-        form_weight(2)
-        scatter_half(0, 1)
-        nc.sync.dma_start(out=da_rows[0], in_=windows[0][:])
-        form_m(2)
-        turn_m(2)
-        stage_a(1, 0)
-        a_last = sb("a_last", T, BF16, tag="m_e_codes1")
-        nc.scalar.activation(out=a_last[:], in_=a_raw[3][:], func=COPY)
-        nc.scalar.activation(out=a_got[:, block(3, N)], in_=a_last[:].indirect(offsets[:]), func=COPY)
-        scatter(da_rows, staged, 1)
-        a_turn[3] = weight[3][:, 0 : N // 2].bitcast(BF16)
-        turn_a(3)
-        correlate(3)
-        quantize_m_e(2)
-        grad_a(2)
+        gather(a_got, a_raw, 3)
+        weight[3] = sb("weight3", E, F32, tag="a_raw3")[:]
         form_weight(3)
+        finish_m(2, nc.gpsimd, 1)
+        stage_half(1, 0)
+        turn_a(3)
+        scatter_half(1, 0)
+        turn_m(2)
+        correlate(3)
+        stage_half(1, 1)
+        scatter_half(1, 1)
+        grad_a(2)
         a_weave = sb("a_weave", PACK * N, BF16, tag="m_e2")
-        weave(nc.scalar.copy, a_weave, a_got, 0)
-        weave(nc.scalar.copy, a_weave, a_got, 1)
-        form_m(3)
-        stage_a(2, 0)
+        scale_c(3, 2)
+        finish_m(3, nc.vector, 2)
+        stage_half(2, 0)
         turn_m(3)
-        stage_a(2, 1)
-        quantize(a_d_codes[:], a_d_scales[:], a_weave[:], E4M3)
+        for part in range(PACK):
+            weave(nc.scalar.copy, a_weave, a_got, part, PACK)
         scatter_half(2, 0)
-        quantize_m_e(3)
         grad_a(3)
-        stage_a(3, 0)
-        stage_a(3, 1)
-        weave(nc.scalar.copy, m_weave, m_rows[:], 0)
-        weave(nc.scalar.copy, m_weave, m_rows[:], 1)
+        stage_half(2, 1)
+        quantize(a_d_codes[:], a_d_scales[:], a_weave[:], E4M3)
         scatter_half(2, 1)
-        nc.sync.dma_start(out=da_rows[2], in_=windows[2][:])
+        for part in range(PACK):
+            weave(nc.scalar.copy, m_weave, m_rows[:], part, PACK)
+        stage_a(3)
         grad_b(0)
         grad_b(1)
         scatter(da_rows, staged, 3)

@@ -45,27 +45,30 @@ def tile_attend_gbarlow_ab_kernel(tc, aT, bT, tg, wm, ca, cb, offs, out_0, out_1
         a_raw, b_raw = planes("a_raw", T, F32), planes("b_raw", T, F32)
         wm_raw = planes("wm_raw", E, F32)
         ca_col, cb_col = sb("ca_col", PACK, F32), sb("cb_col", PACK, F32)
-        cb_row, scale2 = sb("cb_row", E, F32), sb("scale2", E, F32)
+        cb_row = sb("cb_row", E, F32)
+        scale = {t: sb("scale" + str(t), E, F32) for t in range(2, PACK)}
         got = sb("got", 8 * N, BF16)
         b_got, a_got = got[:, block(0, PACK * N)], got[:, block(1, PACK * N)]
         tg_raw = [tile[:] for tile in planes("tg_raw", E, F32)]
         a_turn = [got[:, block(5, N)]] + [sb("a_turn" + str(t), N, BF16)[:] for t in range(1, PACK)]
         b_turn = {0: got[:, block(2, N)], 1: got[:, block(3, N)], 2: got[:, block(4, N)]}
-        a_i_codes, a_i_scales = planes("a_i_codes", P, U32), planes("a_i_scales", P, U8)
+        a_i_codes = {t: sb("a_i_codes" + str(t), P, U32) for t in range(PACK - 1)}
+        a_i_scales = planes("a_i_scales", P, U8)
         b_i_codes, b_i_scales = sb("b_i_codes", E, U32), sb("b_i_scales", E, U8)
         b_weave = sb("b_weave", PACK * N, BF16)
+        a_weave = sb("a_weave", PACK * N, BF16)
         a_d_codes, a_d_scales = sb("a_d_codes", N, U32), sb("a_d_scales", N, U8)
         b_e_scales = sb("b_e_scales", N, U8)
         weight = {}
-        residual = {t: sb("residual" + str(t), E, F32)[:] for t in range(1, PACK)}
+        residual = {3: sb("residual3", E, F32)[:]}
         m_rows = sb("m_rows", PACK * E, BF16)
-        second = sb("second", N // 2, F32)
-        m_e = [sb("m_e0", E, BF16)[:], got[:, block(7, N)], sb("m_e2", E, BF16)[:], second[:].bitcast(BF16)]
-        staged = {3: m_rows[:, 0 : 2 * N].bitcast(F32)}
-        staged_half = {1: [sb("staged1" + h, N // 2, F32)[:] for h in "ab"], 2: [tg_raw[3][:, 0 : N // 2], second[:]]}
-        m_e_codes = {t: sb("m_e_codes" + str(t), P, U32) for t in range(1, PACK)}
+        m_e = {0: sb("m_e0", E, BF16)[:], 2: m_rows[:, block(3, E)]}
+        staged = {3: sb("staged3", N, F32)[:]}
+        staged_half = {}
+        m_e_codes = {t: sb("m_e_codes" + str(t), P, U32) for t in range(2, PACK)}
         m_e_scales = planes("m_e_scales", P, U8)
         m_weave = sb("m_weave", PACK * E, BF16)
+        m_e[3] = m_weave[:, E + E // 2 : 2 * E + E // 2]
         m_d_codes, m_d_scales = sb("m_d_codes", E, U32), sb("m_d_scales", E, U8)
         db = [tile[:] for tile in planes("db", N, F32)]
         windows = planes("window", T, F32)
@@ -73,7 +76,7 @@ def tile_attend_gbarlow_ab_kernel(tc, aT, bT, tg, wm, ca, cb, offs, out_0, out_1
         turn_ps = [psum.tile([P, 512], F32, name="turn_ps" + str(h)) for h in range(2)]
         c_ps = [psum.tile([P, 512], F32, name="c_ps" + str(h)) for h in range(3)]
         cb_ps = psum.tile([P, 512], F32, name="cb_ps")
-        c_bank = (c_ps[0], c_ps[1], c_ps[2], c_ps[0])
+        c_bank = (c_ps[0], c_ps[1], c_ps[2], turn_ps[1])
         grad_ps = [psum.tile([P, 512], F32, name="grad_ps" + str(h)) for h in range(2)]
 
         a_rows, b_rows, wm_rows, tg_rows = rows(aT), rows(bT), rows(wm), rows(tg)
@@ -94,11 +97,12 @@ def tile_attend_gbarlow_ab_kernel(tc, aT, bT, tg, wm, ca, cb, offs, out_0, out_1
         load(tg_raw[0], tg_rows[0])
         load(a_raw[2][:], a_rows[2])
         load(wm_raw[1][:], wm_rows[1])
+        load(wm_raw[2][:], wm_rows[2])
+        load(wm_raw[3][:], wm_rows[3])
         load(tg_raw[1], tg_rows[1])
         load(a_raw[3][:], a_rows[3])
-        for t in range(2, PACK):
-            load(wm_raw[t][:], wm_rows[t])
-            load(tg_raw[t], tg_rows[t])
+        load(tg_raw[2], tg_rows[2])
+        load(tg_raw[3], tg_rows[3])
 
         make_identity(nc, ident[:])
         for t in range(PACK):
@@ -157,6 +161,9 @@ def tile_attend_gbarlow_ab_kernel(tc, aT, bT, tg, wm, ca, cb, offs, out_0, out_1
                 op1=MULT,
             )
 
+        def pool_weight(t):
+            nc.gpsimd.tensor_tensor(out=weight[t], in0=wm_raw[t][:], in1=scale[t][:], op=MULT)
+
         def scale_c(t, parts):
             for part in range(parts):
                 cols = block(part, E // parts)
@@ -169,19 +176,19 @@ def tile_attend_gbarlow_ab_kernel(tc, aT, bT, tg, wm, ca, cb, offs, out_0, out_1
                     op1=MULT,
                 )
 
-        def finish_m(t, engine, parts):
+        def finish_m(t, engine, parts, difference):
             pieces = [block(part, E // parts) for part in range(parts)]
             for cols in pieces:
                 engine.tensor_tensor(
-                    out=residual[t][:, cols], in0=residual[t][:, cols], in1=tg_raw[t][:, cols], op=SUBTRACT
+                    out=difference[:, cols], in0=residual[t][:, cols], in1=tg_raw[t][:, cols], op=SUBTRACT
                 )
             for cols in pieces:
                 engine.tensor_tensor(
-                    out=m_rows[:, block(t, E)][:, cols], in0=residual[t][:, cols], in1=weight[t][:, cols], op=MULT
+                    out=m_rows[:, block(t, E)][:, cols], in0=difference[:, cols], in1=weight[t][:, cols], op=MULT
                 )
 
         def turn_m(t):
-            turn(m_rows[:, block(t, E)], m_e[t], (c_ps[1], c_ps[0], c_ps[0], c_ps[1])[t])
+            turn(m_rows[:, block(t, E)], m_e[t], (c_ps[2], turn_ps[1], c_ps[2], grad_ps[0])[t])
 
         def gradient(bank, codes, scales, moving_codes, moving_scales):
             nc.tensor.matmul_mx(
@@ -205,7 +212,7 @@ def tile_attend_gbarlow_ab_kernel(tc, aT, bT, tg, wm, ca, cb, offs, out_0, out_1
             cols = block(half, E // 2)
             quantize(m_d_codes[:, cols], m_d_scales[:, cols], m_weave[:, block(half, 2 * E)], E5M2)
             for j in range(2 * half, 2 * half + 2):
-                bank = (c_ps[2], turn_ps[0], turn_ps[1], c_ps[0])[j]
+                bank = (c_ps[2], turn_ps[0], turn_ps[1], c_ps[1])[j]
                 gradient(bank, m_d_codes[:, block(j)], m_d_scales[:, block(j)], a_d_codes, a_d_scales)
                 nc.scalar.copy(out=db[j], in_=bank[:])
 
@@ -224,7 +231,8 @@ def tile_attend_gbarlow_ab_kernel(tc, aT, bT, tg, wm, ca, cb, offs, out_0, out_1
         for s in range(PACK):
             nc.tensor.transpose(cb_ps[:, block(s)], cb_col[:, s : s + 1].to_broadcast([P, P]), ident[:])
         nc.scalar.copy(out=in_fours(cb_row[:]), in_=by_e(cb_ps))
-        nc.scalar.activation(out=scale2[:], in_=cb_row[:], func=COPY, scale=ca_col[:, 2:3])
+        for t in range(2, PACK):
+            nc.scalar.activation(out=scale[t][:], in_=cb_row[:], func=COPY, scale=ca_col[:, t : t + 1])
 
         def turn_b(s):
             turn(b_got[:, block(s, N)], b_turn[s], turn_ps[(s + 1) % 2])
@@ -240,8 +248,7 @@ def tile_attend_gbarlow_ab_kernel(tc, aT, bT, tg, wm, ca, cb, offs, out_0, out_1
 
         da_rows, db_rows = rows(out_0), out_1.rearrange("(j q) n -> j q n", q=P)
         gather(a_got, a_raw, 0)
-        after_a0 = sb("after_a0", E + N // 2, F32, tag="a_raw0")
-        weight[0], b_turn[3] = after_a0[:, 0:E], after_a0[:, E : E + N // 2].bitcast(BF16)
+        weight[0], b_turn[3] = got[:, 0 : 2 * N].bitcast(F32), sb("b_turn3", N, BF16, tag="a_raw0")[:]
         form_weight(0)
         turn_b(3)
         b_e_codes = sb("b_e_codes", N, U32, tag="wm_raw0")
@@ -252,55 +259,66 @@ def tile_attend_gbarlow_ab_kernel(tc, aT, bT, tg, wm, ca, cb, offs, out_0, out_1
         residual[0] = sb("residual0", E, F32, tag="a_raw1")[:]
         scale_c(0, 2)
         turn_a(1)
-        finish_m(0, nc.vector, 2)
+        finish_m(0, nc.vector, 2, residual[0])
         turn_m(0)
         correlate(1)
+        after_a1 = sb("after_a1", 2 * E, F32, tag="a_turn1")
+        weight[2], weight[3] = after_a1[:, 0:E], after_a1[:, E : 2 * E]
+        pool_weight(2)
+        pool_weight(3)
         gather(a_got, a_raw, 2)
-        m_e_codes[0] = sb("m_e_codes0", P, U32, tag="a_raw2")
-        grad_a(0)
-        turn_a(2)
-        weight[1] = sb("weight1", E, F32, tag="m_e0")[:]
+        after_a2 = sb("after_a2", 2 * E, F32, tag="a_raw2")
+        weight[1], residual[1] = after_a2[:, 0:E], after_a2[:, E : 2 * E]
         form_weight(1)
+        turn_a(2)
         scale_c(1, 1)
-        staged[0] = sb("staged0", N, F32, tag="wm_raw1")[:]
-        stage_a(0)
+        m_e_codes[0] = sb("m_e_codes0", P, U32, tag="wm_raw1")
+        grad_a(0)
         correlate(2)
-        finish_m(1, nc.gpsimd, 1)
-        weight[2] = sb("weight2", E, F32)[:]
-        nc.gpsimd.tensor_tensor(out=weight[2], in0=wm_raw[2][:], in1=scale2[:], op=MULT)
-        scatter(da_rows, staged, 0)
-        scale_c(2, 1)
-        turn_m(1)
-        grad_a(1)
+        finish_m(1, nc.gpsimd, 1, sb("difference1", E, F32, tag="a_turn2")[:])
         gather(a_got, a_raw, 3)
-        weight[3] = sb("weight3", E, F32, tag="a_raw3")[:]
-        form_weight(3)
-        finish_m(2, nc.gpsimd, 1)
-        stage_half(1, 0)
+        after_a3 = sb("after_a3", N + E, F32, tag="a_raw3")
+        staged_half[0] = [after_a3[:, block(half, N // 2)] for half in range(2)]
+        residual[2] = after_a3[:, N : N + E]
+        scale_c(2, 1)
+        stage_half(0, 0)
+        stage_half(0, 1)
         turn_a(3)
-        scatter_half(1, 0)
-        turn_m(2)
-        correlate(3)
-        stage_half(1, 1)
-        scatter_half(1, 1)
-        grad_a(2)
-        a_weave = sb("a_weave", PACK * N, BF16, tag="m_e2")
-        scale_c(3, 2)
-        finish_m(3, nc.vector, 2)
-        stage_half(2, 0)
-        turn_m(3)
-        for part in range(PACK):
+        scatter_half(0, 0)
+        scatter_half(0, 1)
+        for part in range(PACK - 1):
             weave(nc.scalar.copy, a_weave, a_got, part, PACK)
+        m_e[1] = sb("m_e1", E, BF16)[:]
+        turn_m(1)
+        weave(nc.scalar.copy, a_weave, a_got, PACK - 1, PACK)
+        finish_m(2, nc.gpsimd, 1, residual[2])
+        a_i_codes[3] = sb("a_i_codes3", P, U32, tag="a_raw3")
+        m_e_codes[1] = sb("m_e_codes1", P, U32, tag="tg_raw2")
+        correlate(3)
+        grad_a(1)
+        quantize(a_d_codes[:], a_d_scales[:], a_weave[:], E4M3)
+        scale_c(3, 1)
+        staged_half[1] = [sb("staged1" + half, N // 2, F32)[:] for half in "ab"]
+        stage_half(1, 0)
+        turn_m(2)
+        stage_half(1, 1)
+        scatter_half(1, 0)
+        grad_a(2)
+        finish_m(3, nc.gpsimd, 1, residual[3])
+        scatter_half(1, 1)
+        staged_half[2] = [sb("staged2a", N // 2, F32)[:], sb("staged2b", N // 2, F32)[:]]
+        stage_half(2, 0)
         scatter_half(2, 0)
+        weave(nc.scalar.copy, m_weave, m_rows[:], 0, PACK)
+        turn_m(3)
         grad_a(3)
         stage_half(2, 1)
-        quantize(a_d_codes[:], a_d_scales[:], a_weave[:], E4M3)
         scatter_half(2, 1)
-        for part in range(PACK):
-            weave(nc.scalar.copy, m_weave, m_rows[:], part, PACK)
+        weave(nc.scalar.copy, m_weave, m_rows[:], 1, PACK)
         stage_a(3)
+        weave(nc.scalar.copy, m_weave, m_rows[:], 1, 2)
         grad_b(0)
-        grad_b(1)
         scatter(da_rows, staged, 3)
+        grad_b(1)
         for j in range(PACK):
             scatter(db_rows, db, j)

@@ -46,28 +46,29 @@ def tile_attend_gbarlow_ab_kernel(tc, aT, bT, tg, wm, ca, cb, offs, out_0, out_1
         wm_raw = planes("wm_raw", E, F32)
         ca_col, cb_col = sb("ca_col", PACK, F32), sb("cb_col", PACK, F32)
         cb_row = sb("cb_row", E, F32)
-        scale = {t: sb("scale" + str(t), E, F32) for t in range(2, PACK)}
-        got = sb("got", 8 * N, BF16)
+        scale2 = sb("scale2", E, F32)
+        got = sb("got", 9 * N, BF16)
         b_got, a_got = got[:, block(0, PACK * N)], got[:, block(1, PACK * N)]
         tg_raw = [tile[:] for tile in planes("tg_raw", E, F32)]
-        a_turn = [got[:, block(5, N)]] + [sb("a_turn" + str(t), N, BF16)[:] for t in range(1, PACK)]
+        a_turn = [sb("a_turn" + str(t), N, BF16)[:] for t in range(PACK - 1)]
         b_turn = {0: got[:, block(2, N)], 1: got[:, block(3, N)], 2: got[:, block(4, N)]}
         a_i_codes = {t: sb("a_i_codes" + str(t), P, U32) for t in range(PACK - 1)}
         a_i_scales = planes("a_i_scales", P, U8)
         b_i_codes, b_i_scales = sb("b_i_codes", E, U32), sb("b_i_scales", E, U8)
-        b_weave = sb("b_weave", PACK * N, BF16)
-        a_weave = sb("a_weave", PACK * N, BF16)
-        a_d_codes, a_d_scales = sb("a_d_codes", N, U32), sb("a_d_scales", N, U8)
+        b_weave = got[:, 5 * N : 9 * N]
+        a_weave = sb("a_weave", PACK * N, BF16)[:]
+        a_d_scales = sb("a_d_scales", N, U8)
         b_e_scales = sb("b_e_scales", N, U8)
         weight = {}
         residual = {3: sb("residual3", E, F32)[:]}
         m_rows = sb("m_rows", PACK * E, BF16)
+        a_turn.append(m_rows[:, block(2, E)])
         m_e = {0: sb("m_e0", E, BF16)[:], 2: m_rows[:, block(3, E)]}
         staged = {3: sb("staged3", N, F32)[:]}
         staged_half = {}
-        m_e_codes = {t: sb("m_e_codes" + str(t), P, U32) for t in range(2, PACK)}
+        m_e_codes = {t: sb("m_e_codes" + str(t), P, U32) for t in range(1, PACK)}
         m_e_scales = planes("m_e_scales", P, U8)
-        m_weave = sb("m_weave", PACK * E, BF16)
+        m_weave = sb("m_weave", PACK * E, BF16)[:]
         m_e[3] = m_weave[:, E + E // 2 : 2 * E + E // 2]
         m_d_codes, m_d_scales = sb("m_d_codes", E, U32), sb("m_d_scales", E, U8)
         db = [tile[:] for tile in planes("db", N, F32)]
@@ -76,7 +77,7 @@ def tile_attend_gbarlow_ab_kernel(tc, aT, bT, tg, wm, ca, cb, offs, out_0, out_1
         turn_ps = [psum.tile([P, 512], F32, name="turn_ps" + str(h)) for h in range(2)]
         c_ps = [psum.tile([P, 512], F32, name="c_ps" + str(h)) for h in range(3)]
         cb_ps = psum.tile([P, 512], F32, name="cb_ps")
-        c_bank = (c_ps[0], c_ps[1], c_ps[2], turn_ps[1])
+        c_bank = (c_ps[0], c_ps[1], c_ps[2], c_ps[0])
         grad_ps = [psum.tile([P, 512], F32, name="grad_ps" + str(h)) for h in range(2)]
 
         a_rows, b_rows, wm_rows, tg_rows = rows(aT), rows(bT), rows(wm), rows(tg)
@@ -98,9 +99,9 @@ def tile_attend_gbarlow_ab_kernel(tc, aT, bT, tg, wm, ca, cb, offs, out_0, out_1
         load(a_raw[2][:], a_rows[2])
         load(wm_raw[1][:], wm_rows[1])
         load(wm_raw[2][:], wm_rows[2])
-        load(wm_raw[3][:], wm_rows[3])
         load(tg_raw[1], tg_rows[1])
         load(a_raw[3][:], a_rows[3])
+        load(wm_raw[3][:], wm_rows[3])
         load(tg_raw[2], tg_rows[2])
         load(tg_raw[3], tg_rows[3])
 
@@ -129,7 +130,7 @@ def tile_attend_gbarlow_ab_kernel(tc, aT, bT, tg, wm, ca, cb, offs, out_0, out_1
         def weave(copy, woven, source, part, parts):
             cols = block(part, N // PACK // parts)
             copy(
-                out=woven[:].rearrange("p (c i t) -> p c t i", i=4, t=PACK)[:, cols],
+                out=woven.rearrange("p (c i t) -> p c t i", i=4, t=PACK)[:, cols],
                 in_=source.rearrange("p (t c i) -> p c t i", i=4, t=PACK)[:, cols],
             )
 
@@ -161,9 +162,6 @@ def tile_attend_gbarlow_ab_kernel(tc, aT, bT, tg, wm, ca, cb, offs, out_0, out_1
                 op1=MULT,
             )
 
-        def pool_weight(t):
-            nc.gpsimd.tensor_tensor(out=weight[t], in0=wm_raw[t][:], in1=scale[t][:], op=MULT)
-
         def scale_c(t, parts):
             for part in range(parts):
                 cols = block(part, E // parts)
@@ -188,7 +186,7 @@ def tile_attend_gbarlow_ab_kernel(tc, aT, bT, tg, wm, ca, cb, offs, out_0, out_1
                 )
 
         def turn_m(t):
-            turn(m_rows[:, block(t, E)], m_e[t], (c_ps[2], turn_ps[1], c_ps[2], grad_ps[0])[t])
+            turn(m_rows[:, block(t, E)], m_e[t], (c_ps[2], grad_ps[0], grad_ps[1], grad_ps[0])[t])
 
         def gradient(bank, codes, scales, moving_codes, moving_scales):
             nc.tensor.matmul_mx(
@@ -231,8 +229,7 @@ def tile_attend_gbarlow_ab_kernel(tc, aT, bT, tg, wm, ca, cb, offs, out_0, out_1
         for s in range(PACK):
             nc.tensor.transpose(cb_ps[:, block(s)], cb_col[:, s : s + 1].to_broadcast([P, P]), ident[:])
         nc.scalar.copy(out=in_fours(cb_row[:]), in_=by_e(cb_ps))
-        for t in range(2, PACK):
-            nc.scalar.activation(out=scale[t][:], in_=cb_row[:], func=COPY, scale=ca_col[:, t : t + 1])
+        nc.scalar.activation(out=scale2[:], in_=cb_row[:], func=COPY, scale=ca_col[:, 2:3])
 
         def turn_b(s):
             turn(b_got[:, block(s, N)], b_turn[s], turn_ps[(s + 1) % 2])
@@ -252,23 +249,21 @@ def tile_attend_gbarlow_ab_kernel(tc, aT, bT, tg, wm, ca, cb, offs, out_0, out_1
         form_weight(0)
         turn_b(3)
         b_e_codes = sb("b_e_codes", N, U32, tag="wm_raw0")
-        quantize(b_e_codes[:], b_e_scales[:], b_weave[:], E4M3)
+        quantize(b_e_codes[:], b_e_scales[:], b_weave, E4M3)
         turn_a(0)
         correlate(0)
         gather(a_got, a_raw, 1)
-        residual[0] = sb("residual0", E, F32, tag="a_raw1")[:]
+        residual[0] = sb("residual0", E, F32)[:]
         scale_c(0, 2)
         turn_a(1)
         finish_m(0, nc.vector, 2, residual[0])
         turn_m(0)
         correlate(1)
         after_a1 = sb("after_a1", 2 * E, F32, tag="a_turn1")
-        weight[2], weight[3] = after_a1[:, 0:E], after_a1[:, E : 2 * E]
-        pool_weight(2)
-        pool_weight(3)
+        weight[1], weight[2] = after_a1[:, 0:E], after_a1[:, E : 2 * E]
+        nc.gpsimd.tensor_tensor(out=weight[2], in0=wm_raw[2][:], in1=scale2[:], op=MULT)
         gather(a_got, a_raw, 2)
-        after_a2 = sb("after_a2", 2 * E, F32, tag="a_raw2")
-        weight[1], residual[1] = after_a2[:, 0:E], after_a2[:, E : 2 * E]
+        residual[1] = sb("residual1", E, F32, tag="a_raw2")[:]
         form_weight(1)
         turn_a(2)
         scale_c(1, 1)
@@ -277,31 +272,32 @@ def tile_attend_gbarlow_ab_kernel(tc, aT, bT, tg, wm, ca, cb, offs, out_0, out_1
         correlate(2)
         finish_m(1, nc.gpsimd, 1, sb("difference1", E, F32, tag="a_turn2")[:])
         gather(a_got, a_raw, 3)
-        after_a3 = sb("after_a3", N + E, F32, tag="a_raw3")
-        staged_half[0] = [after_a3[:, block(half, N // 2)] for half in range(2)]
-        residual[2] = after_a3[:, N : N + E]
+        after_a3 = sb("after_a3", N // 2 + 2 * E, F32, tag="a_raw3")
+        residual[2], weight[3] = after_a3[:, 0:E], after_a3[:, E : 2 * E]
+        staged_half[0] = [after_a3[:, 2 * E : 2 * E + N // 2], sb("staged0b", N // 2, F32)[:]]
+        staged_half[1] = [sb("staged1" + half, N // 2, F32)[:] for half in "ab"]
         scale_c(2, 1)
+        form_weight(3)
         stage_half(0, 0)
-        stage_half(0, 1)
         turn_a(3)
         scatter_half(0, 0)
-        scatter_half(0, 1)
-        for part in range(PACK - 1):
-            weave(nc.scalar.copy, a_weave, a_got, part, PACK)
         m_e[1] = sb("m_e1", E, BF16)[:]
         turn_m(1)
-        weave(nc.scalar.copy, a_weave, a_got, PACK - 1, PACK)
-        finish_m(2, nc.gpsimd, 1, residual[2])
-        a_i_codes[3] = sb("a_i_codes3", P, U32, tag="a_raw3")
-        m_e_codes[1] = sb("m_e_codes1", P, U32, tag="tg_raw2")
+        stage_half(0, 1)
+        nc.gpsimd.tensor_tensor(out=residual[2], in0=residual[2], in1=tg_raw[2], op=SUBTRACT)
+        a_i_codes[3] = sb("a_i_codes3", P, U32, tag="tg_raw2")
         correlate(3)
         grad_a(1)
-        quantize(a_d_codes[:], a_d_scales[:], a_weave[:], E4M3)
+        nc.gpsimd.tensor_tensor(out=m_rows[:, block(2, E)], in0=residual[2], in1=weight[2], op=MULT)
+        scatter_half(0, 1)
         scale_c(3, 1)
-        staged_half[1] = [sb("staged1" + half, N // 2, F32)[:] for half in "ab"]
         stage_half(1, 0)
+        for part in range(PACK):
+            weave(nc.scalar.copy, a_weave, a_got, part, PACK)
         turn_m(2)
         stage_half(1, 1)
+        a_d_codes = sb("a_d_codes", N, U32, tag="a_turn1")
+        quantize(a_d_codes[:], a_d_scales[:], a_weave, E4M3)
         scatter_half(1, 0)
         grad_a(2)
         finish_m(3, nc.gpsimd, 1, residual[3])

@@ -113,19 +113,32 @@ def tile_attend_gbarlow_ab_kernel(tc, aT, bT, tg, wm, ca, cb, offs, out_0, out_1
             nc.vector.quantize_mx(out=codes.bitcast(fmt), scales=scales, in_=values)
 
         def gather(target, raw, t):
-            nc.vector.tensor_copy(target[:, block(t, N)], raw[t][:].indirect(offsets[:]))
-
-        def turn(source, turned, bank):
-            words = source.bitcast(F32)
-            for u in range(2):
-                nc.tensor.transpose(bank[:, block(u)], words[:, u : 2 * P : 2], ident[:])
-            nc.scalar.copy(
-                out=turned.bitcast(F32).rearrange("j (r u) -> j r u", u=2),
-                in_=bank[:, 0 : 2 * P].rearrange("j (u r) -> j r u", u=2),
+            nc.vector.tensor_copy(
+                target[:, block(t, N)].rearrange("p (u g j) -> p g u j", u=2, j=16), raw[t][:].indirect(offsets[:])
             )
 
+        def turn(words, turned, bank):
+            for u in range(2):
+                nc.tensor.transpose(bank[:, block(2 * u)], words[u], ident[:])
+            nc.scalar.copy(
+                out=turned.bitcast(F32).rearrange("j (r u) -> j r u", u=2),
+                in_=bank[:].rearrange("j (u r) -> j r u", u=2)[:, 0:P],
+            )
+
+        def word_runs(source):
+            return [source.bitcast(F32)[:, block(u)] for u in range(2)]
+
+        def second_words(source):
+            return [source.bitcast(F32)[:, u : 2 * P : 2] for u in range(2)]
+
+        def by_slot(bank):
+            return bank[:].rearrange("p (u g j) -> p g u j", u=2, j=16)
+
+        def in_runs(x):
+            return x.rearrange("p (g u j) -> p g u j", u=2, j=16)
+
         def turn_a(t):
-            turn(a_got[:, block(t, N)], a_turn[t], turn_ps[t % 2])
+            turn(word_runs(a_got[:, block(t, N)]), a_turn[t], turn_ps[t % 2])
 
         def weave(copy, woven, source, part, parts):
             cols = block(part, N // PACK // parts)
@@ -186,7 +199,7 @@ def tile_attend_gbarlow_ab_kernel(tc, aT, bT, tg, wm, ca, cb, offs, out_0, out_1
                 )
 
         def turn_m(t):
-            turn(m_rows[:, block(t, E)], m_e[t], (c_ps[2], grad_ps[0], grad_ps[1], grad_ps[0])[t])
+            turn(second_words(m_rows[:, block(t, E)]), m_e[t], (c_ps[2], grad_ps[0], grad_ps[1], grad_ps[0])[t])
 
         def gradient(bank, codes, scales, moving_codes, moving_scales):
             nc.tensor.matmul_mx(
@@ -204,7 +217,7 @@ def tile_attend_gbarlow_ab_kernel(tc, aT, bT, tg, wm, ca, cb, offs, out_0, out_1
             gradient(grad_ps[t % 2], m_e_codes[t][:], m_e_scales[t][:], b_e_codes, b_e_scales)
 
         def stage_a(t):
-            nc.scalar.copy(out=staged[t], in_=grad_ps[t % 2][:])
+            nc.scalar.copy(out=in_runs(staged[t]), in_=by_slot(grad_ps[t % 2]))
 
         def grad_b(half):
             cols = block(half, E // 2)
@@ -212,10 +225,10 @@ def tile_attend_gbarlow_ab_kernel(tc, aT, bT, tg, wm, ca, cb, offs, out_0, out_1
             for j in range(2 * half, 2 * half + 2):
                 bank = (c_ps[2], turn_ps[0], turn_ps[1], c_ps[1])[j]
                 gradient(bank, m_d_codes[:, block(j)], m_d_scales[:, block(j)], a_d_codes, a_d_scales)
-                nc.scalar.copy(out=db[j], in_=bank[:])
+                nc.scalar.copy(out=in_runs(db[j]), in_=by_slot(bank))
 
         def stage_half(t, half):
-            nc.scalar.copy(out=staged_half[t][half], in_=grad_ps[t % 2][:, block(half, N // 2)])
+            nc.scalar.copy(out=in_runs(staged_half[t][half]), in_=by_slot(grad_ps[t % 2])[:, block(half, N // 64)])
 
         def scatter_half(t, half):
             nc.vector.tensor_copy(windows[t][:].indirect(offsets[:, block(half, N // 32)]), staged_half[t][half])
@@ -232,7 +245,7 @@ def tile_attend_gbarlow_ab_kernel(tc, aT, bT, tg, wm, ca, cb, offs, out_0, out_1
         nc.scalar.activation(out=scale2[:], in_=cb_row[:], func=COPY, scale=ca_col[:, 2:3])
 
         def turn_b(s):
-            turn(b_got[:, block(s, N)], b_turn[s], turn_ps[(s + 1) % 2])
+            turn(word_runs(b_got[:, block(s, N)]), b_turn[s], turn_ps[(s + 1) % 2])
             quantize(b_i_codes[:, block(s)], b_i_scales[:, block(s)], b_turn[s], E4M3)
 
         for s in range(PACK):

@@ -29,7 +29,7 @@ def tile_attend_gbarlow_ab_kernel(tc, aT, bT, tg, wm, ca, cb, offs, out_0, out_1
         psum = ctx.enter_context(tc.psum_pool(name="psum", bufs=1))
 
         def sb(name, width, dtype, tag=None):
-            return keep.tile([P, width], dtype, name=name, tag=tag or name, align_bytes=64)
+            return keep.tile([P, width], dtype, name=name, tag=tag or name, align_bytes=256)
 
         def planes(name, width, dtype):
             return [sb(name + str(t), width, dtype) for t in range(PACK)]

@@ -20,6 +20,8 @@ SUBTRACT = mybir.AluOpType.subtract
 
 P = 128
 PACK = 4
+WINDOWS = 5
+SPLIT = 192
 
 
 def tile_attend_gbarlow_ab_kernel(tc, aT, bT, tg, wm, ca, cb, offs, out_0, out_1):
@@ -29,10 +31,10 @@ def tile_attend_gbarlow_ab_kernel(tc, aT, bT, tg, wm, ca, cb, offs, out_0, out_1
         psum = ctx.enter_context(tc.psum_pool(name="psum", bufs=1))
 
         def sb(name, width, dtype, tag=None):
-            return keep.tile([P, width], dtype, name=name, tag=tag or name, align_bytes=256)
+            return keep.tile([P, width], dtype, name=name, tag=tag or name, align_bytes=256)[:]
 
-        def planes(name, width, dtype):
-            return [sb(name + str(t), width, dtype) for t in range(PACK)]
+        def planes(name, width, dtype, count=PACK):
+            return [sb(name + str(t), width, dtype) for t in range(count)]
 
         def block(t, width=P):
             return slice(t * width, (t + 1) * width)
@@ -40,294 +42,302 @@ def tile_attend_gbarlow_ab_kernel(tc, aT, bT, tg, wm, ca, cb, offs, out_0, out_1
         def rows(x):
             return x.rearrange("(p t) n -> t p n", t=PACK)
 
+        def bank(name):
+            return psum.tile([P, 512], F32, name=name)[:]
+
         offsets = keep.tile([P, N // 16], U16, name="offsets")
         ident = sb("ident", P, F32)
         a_raw, b_raw = planes("a_raw", T, F32), planes("b_raw", T, F32)
-        wm_raw = planes("wm_raw", E, F32)
+        wm_raw, tg_raw = planes("wm_raw", E, F32), planes("tg_raw", E, F32)
         ca_col, cb_col = sb("ca_col", PACK, F32), sb("cb_col", PACK, F32)
         cb_row = sb("cb_row", E, F32)
-        scale2 = sb("scale2", E, F32)
-        got = sb("got", 9 * N, BF16)
-        b_got, a_got = got[:, block(0, PACK * N)], got[:, block(1, PACK * N)]
-        tg_raw = [tile[:] for tile in planes("tg_raw", E, F32)]
-        a_turn = [sb("a_turn" + str(t), N, BF16)[:] for t in range(PACK - 1)]
-        b_turn = {0: got[:, block(2, N)], 1: got[:, block(3, N)], 2: got[:, block(4, N)]}
-        a_i_codes = {t: sb("a_i_codes" + str(t), P, U32) for t in range(PACK - 1)}
+        scale = {t: sb("scale" + str(t), E, F32) for t in range(1, PACK)}
+        a_start = PACK * N - N // 2
+        got = sb("got", a_start + PACK * 2 * N, BF16)
+        b_planes = got[:, 0 : PACK * N].rearrange("p (t x) -> p t x", t=PACK)
+        a_planes = got[:, a_start:].rearrange("p (t x) -> p t x", t=PACK)[:, :, 0:N]
+        b_got = [got[:, block(s, N)] for s in range(PACK)]
+        a_got = [got[:, a_start:][:, block(2 * t, N)] for t in range(PACK)]
+        b_turn = planes("b_turn", N, BF16)
+        a_i_codes = {t: sb("a_i_codes" + str(t), P, U32) for t in (0, 3)}
         a_i_scales = planes("a_i_scales", P, U8)
         b_i_codes, b_i_scales = sb("b_i_codes", E, U32), sb("b_i_scales", E, U8)
-        b_weave = got[:, 5 * N : 9 * N]
-        a_weave = sb("a_weave", PACK * N, BF16)[:]
-        a_d_scales = sb("a_d_scales", N, U8)
-        b_e_scales = sb("b_e_scales", N, U8)
+        a_weave, b_weave = sb("a_weave", PACK * N, BF16), sb("b_weave", PACK * N, BF16)
+        a_d_codes, a_d_scales = sb("a_d_codes", N, U32), sb("a_d_scales", N, U8)
+        b_e_codes, b_e_scales = sb("b_e_codes", N, U32), sb("b_e_scales", N, U8)
+        a_turn = [a_got[1], sb("a_turn1", N, BF16), sb("a_turn2", N, BF16), a_weave[:, N + N // 2 : 2 * N + N // 2]]
         weight = {}
-        residual = {3: sb("residual3", E, F32)[:]}
+        residual = {t: got[:, a_start:][:, block(t + 2, 2 * N)].bitcast(F32) for t in range(2)}
+        residual[3] = sb("residual3", E, F32)
         m_rows = sb("m_rows", PACK * E, BF16)
-        a_turn.append(m_rows[:, block(2, E)])
-        m_e = {0: sb("m_e0", E, BF16)[:], 2: m_rows[:, block(3, E)]}
-        staged = {3: sb("staged3", N, F32)[:]}
-        staged_half = {}
+        m_planes = m_rows.rearrange("p (t x) -> p t x", t=PACK)
+        m_e = {t: sb("m_e" + str(t), E, BF16) for t in (0, 2, 3)}
         m_e_codes = {t: sb("m_e_codes" + str(t), P, U32) for t in range(1, PACK)}
         m_e_scales = planes("m_e_scales", P, U8)
-        m_weave = sb("m_weave", PACK * E, BF16)[:]
-        m_e[3] = m_weave[:, E + E // 2 : 2 * E + E // 2]
-        m_d_codes, m_d_scales = sb("m_d_codes", E, U32), sb("m_d_scales", E, U8)
-        db = [tile[:] for tile in planes("db", N, F32)]
-        windows = planes("window", T, F32)
+        m_weave = sb("m_weave", PACK * E, BF16)
+        m_d_codes, m_d_scales = planes("m_d_codes", P, U32), planes("m_d_scales", P, U8)
+        da, db = planes("da", N, F32), planes("db", N, F32)
+        windows = planes("window", T, F32, WINDOWS)
 
-        turn_ps = [psum.tile([P, 512], F32, name="turn_ps" + str(h)) for h in range(2)]
-        c_ps = [psum.tile([P, 512], F32, name="c_ps" + str(h)) for h in range(3)]
-        cb_ps = psum.tile([P, 512], F32, name="cb_ps")
-        c_bank = (c_ps[0], c_ps[1], c_ps[2], c_ps[0])
-        grad_ps = [psum.tile([P, 512], F32, name="grad_ps" + str(h)) for h in range(2)]
+        cb_ps = bank("cb_ps")
+        turn_ps = [bank("turn_ps0"), bank("turn_ps1")]
+        c_ps = [bank("c_ps0"), bank("c_ps1")]
+        grad_ps = [bank("grad_ps0"), bank("grad_ps1"), bank("grad_ps2")]
 
         a_rows, b_rows, wm_rows, tg_rows = rows(aT), rows(bT), rows(wm), rows(tg)
+        da_rows, db_rows = rows(out_0), out_1.rearrange("(j q) n -> j q n", q=P)
 
         def load(tile, source):
             nc.sync.dma_start(out=tile, in_=source)
 
-        load(b_raw[0][:], b_rows[0])
-        nc.sync.dma_start(offsets[:], offs)
-        nc.scalar.dma_start(out=cb_col[:], in_=cb[0:1, :].rearrange("o (q s) -> q (o s)", s=PACK))
-        load(b_raw[1][:], b_rows[1])
-        nc.scalar.dma_start(out=ca_col[:], in_=ca.rearrange("(p t) o -> p (t o)", t=PACK))
-        load(b_raw[2][:], b_rows[2])
-        load(b_raw[3][:], b_rows[3])
-        load(a_raw[0][:], a_rows[0])
-        load(wm_raw[0][:], wm_rows[0])
-        load(a_raw[1][:], a_rows[1])
-        load(tg_raw[0], tg_rows[0])
-        load(a_raw[2][:], a_rows[2])
-        load(wm_raw[1][:], wm_rows[1])
-        load(wm_raw[2][:], wm_rows[2])
-        load(tg_raw[1], tg_rows[1])
-        load(a_raw[3][:], a_rows[3])
-        load(wm_raw[3][:], wm_rows[3])
-        load(tg_raw[2], tg_rows[2])
-        load(tg_raw[3], tg_rows[3])
+        def load_w(t):
+            load(wm_raw[t], wm_rows[t])
+            load(tg_raw[t], tg_rows[t])
 
-        make_identity(nc, ident[:])
-        for t in range(PACK):
-            (nc.vector if t < 2 else nc.gpsimd).memset(windows[t][:].bitcast(I32), 0)
+        load(b_raw[0], b_rows[0])
+        nc.sync.dma_start(offsets[:], offs)
+        nc.scalar.dma_start(out=cb_col, in_=cb[0:1, :].rearrange("o (q s) -> q (o s)", s=PACK))
+        load(b_raw[1], b_rows[1])
+        nc.scalar.dma_start(out=ca_col, in_=ca.rearrange("(p t) o -> p (t o)", t=PACK))
+        load(b_raw[2], b_rows[2])
+        load(b_raw[3], b_rows[3])
+        load(a_raw[0], a_rows[0])
+        load_w(0)
+        load(a_raw[1], a_rows[1])
+        load(a_raw[2], a_rows[2])
+        load_w(1)
+        load(a_raw[3], a_rows[3])
+        load_w(2)
+        load_w(3)
+
+        make_identity(nc, ident)
+        for k in range(WINDOWS):
+            (nc.vector if k < 2 else nc.gpsimd).memset(windows[k].bitcast(I32), 0)
+
+        def vector_copy(out, in_):
+            nc.vector.tensor_copy(out, in_)
+
+        def scalar_copy(out, in_):
+            nc.scalar.copy(out=out, in_=in_)
+
+        def scalar_move(out, in_):
+            nc.scalar.activation(out, in_, COPY)
+
+        def part_of_list(part, parts):
+            return offsets[:, block(part, N // 16 // parts)]
 
         def quantize(codes, scales, values, fmt):
             nc.vector.quantize_mx(out=codes.bitcast(fmt), scales=scales, in_=values)
 
-        def gather(target, raw, t):
-            nc.vector.tensor_copy(
-                target[:, block(t, N)].rearrange("p (u g j) -> p g u j", u=2, j=16), raw[t][:].indirect(offsets[:])
-            )
+        def gather(move, target, raw, first=0, last=N):
+            move(target[:, first:last], raw.indirect(offsets[:, first // 16 : last // 16]))
 
-        def turn(words, turned, bank):
+        def turn(source, into):
             for u in range(2):
-                nc.tensor.transpose(bank[:, block(2 * u)], words[u], ident[:])
-            nc.scalar.copy(
-                out=turned.bitcast(F32).rearrange("j (r u) -> j r u", u=2),
-                in_=bank[:].rearrange("j (u r) -> j r u", u=2)[:, 0:P],
+                nc.tensor.transpose(into[:, block(2 * u)], source.bitcast(F32)[:, u : 2 * P : 2], ident)
+
+        def turned(copy, target, source):
+            copy(
+                target.bitcast(F32).rearrange("j (r u) -> j r u", u=2),
+                source.rearrange("j (u r) -> j r u", u=2)[:, 0:P],
             )
-
-        def word_runs(source):
-            return [source.bitcast(F32)[:, block(u)] for u in range(2)]
-
-        def second_words(source):
-            return [source.bitcast(F32)[:, u : 2 * P : 2] for u in range(2)]
-
-        def by_slot(bank):
-            return bank[:].rearrange("p (u g j) -> p g u j", u=2, j=16)
-
-        def in_runs(x):
-            return x.rearrange("p (g u j) -> p g u j", u=2, j=16)
-
-        def turn_a(t):
-            turn(word_runs(a_got[:, block(t, N)]), a_turn[t], turn_ps[t % 2])
 
         def weave(copy, woven, source, part, parts):
             cols = block(part, N // PACK // parts)
             copy(
-                out=woven.rearrange("p (c i t) -> p c t i", i=4, t=PACK)[:, cols],
-                in_=source.rearrange("p (t c i) -> p c t i", i=4, t=PACK)[:, cols],
+                woven.rearrange("p (c i t) -> p c t i", i=4, t=PACK)[:, cols],
+                source.rearrange("p t (c i) -> p c t i", i=4)[:, cols],
             )
 
-        def correlate(t):
-            quantize(a_i_codes[t][:], a_i_scales[t][:], a_turn[t], E4M3)
+        def product(into, codes, scales, fmt, moving_codes, moving_scales):
             nc.tensor.matmul_mx(
-                out=c_bank[t][:],
-                lhsT=a_i_codes[t][:].bitcast(E4M3),
-                lhsT_scale=a_i_scales[t][:],
-                rhs=b_i_codes[:].bitcast(E4M3),
-                rhs_scale=b_i_scales[:],
+                out=into,
+                lhsT=codes.bitcast(fmt),
+                lhsT_scale=scales,
+                rhs=moving_codes.bitcast(E4M3),
+                rhs_scale=moving_scales,
                 start=True,
                 stop=True,
             )
 
-        def by_e(bank):
-            return bank[:].rearrange("p (s q) -> p q s", s=PACK)
+        def by_e(source):
+            return source.rearrange("p (s q) -> p q s", s=PACK)
 
         def in_fours(x):
             return x.rearrange("p (q s) -> p q s", s=PACK)
 
-        def form_weight(t):
+        def turn_a(t, copy):
+            turn(a_got[t], turn_ps[t % 2])
+            turned(copy, a_turn[t], turn_ps[t % 2])
+
+        def correlate(t):
+            quantize(a_i_codes[t], a_i_scales[t], a_turn[t], E4M3)
+            product(c_ps[t % 2], a_i_codes[t], a_i_scales[t], E4M3, b_i_codes, b_i_scales)
+
+        def weight_on_vector(t):
             nc.vector.scalar_tensor_tensor(
                 out=in_fours(weight[t]),
-                in0=in_fours(wm_raw[t][:]),
+                in0=in_fours(wm_raw[t]),
                 scalar=ca_col[:, t : t + 1],
                 in1=by_e(cb_ps),
                 op0=MULT,
                 op1=MULT,
             )
 
+        def weight_on_gpsimd(t):
+            nc.gpsimd.tensor_tensor(out=weight[t], in0=wm_raw[t], in1=scale[t], op=MULT)
+
         def scale_c(t, parts):
             for part in range(parts):
                 cols = block(part, E // parts)
                 nc.vector.scalar_tensor_tensor(
                     out=in_fours(residual[t][:, cols]),
-                    in0=by_e(c_bank[t])[:, block(part, P // parts)],
+                    in0=by_e(c_ps[t % 2])[:, block(part, P // parts)],
                     scalar=ca_col[:, t : t + 1],
                     in1=in_fours(cb_row[:, cols]),
                     op0=MULT,
                     op1=MULT,
                 )
 
-        def finish_m(t, engine, parts, difference):
-            pieces = [block(part, E // parts) for part in range(parts)]
-            for cols in pieces:
+        def subtract(t, engine, parts):
+            for part in range(parts):
+                cols = block(part, E // parts)
                 engine.tensor_tensor(
-                    out=difference[:, cols], in0=residual[t][:, cols], in1=tg_raw[t][:, cols], op=SUBTRACT
-                )
-            for cols in pieces:
-                engine.tensor_tensor(
-                    out=m_rows[:, block(t, E)][:, cols], in0=difference[:, cols], in1=weight[t][:, cols], op=MULT
+                    out=residual[t][:, cols], in0=residual[t][:, cols], in1=tg_raw[t][:, cols], op=SUBTRACT
                 )
 
-        def turn_m(t):
-            turn(second_words(m_rows[:, block(t, E)]), m_e[t], (c_ps[2], grad_ps[0], grad_ps[1], grad_ps[0])[t])
+        def weigh(t, engine, parts):
+            for part in range(parts):
+                cols = block(part, E // parts)
+                engine.tensor_tensor(
+                    out=m_rows[:, block(t, E)][:, cols], in0=residual[t][:, cols], in1=weight[t][:, cols], op=MULT
+                )
 
-        def gradient(bank, codes, scales, moving_codes, moving_scales):
-            nc.tensor.matmul_mx(
-                out=bank[:],
-                lhsT=codes.bitcast(E5M2),
-                lhsT_scale=scales,
-                rhs=moving_codes[:].bitcast(E4M3),
-                rhs_scale=moving_scales[:],
-                start=True,
-                stop=True,
-            )
+        def turn_m(t, copy):
+            turn(m_rows[:, block(t, E)], grad_ps[t % 3])
+            turned(copy, m_e[t], grad_ps[t % 3])
 
         def grad_a(t):
-            quantize(m_e_codes[t][:], m_e_scales[t][:], m_e[t], E5M2)
-            gradient(grad_ps[t % 2], m_e_codes[t][:], m_e_scales[t][:], b_e_codes, b_e_scales)
+            quantize(m_e_codes[t], m_e_scales[t], m_e[t], E5M2)
+            product(grad_ps[t % 3], m_e_codes[t], m_e_scales[t], E5M2, b_e_codes, b_e_scales)
 
-        def stage_a(t):
-            nc.scalar.copy(out=in_runs(staged[t]), in_=by_slot(grad_ps[t % 2]))
+        db_ps = (turn_ps[0], c_ps[0], cb_ps, turn_ps[1])
 
-        def grad_b(half):
-            cols = block(half, E // 2)
-            quantize(m_d_codes[:, cols], m_d_scales[:, cols], m_weave[:, block(half, 2 * E)], E5M2)
-            for j in range(2 * half, 2 * half + 2):
-                bank = (c_ps[2], turn_ps[0], turn_ps[1], c_ps[1])[j]
-                gradient(bank, m_d_codes[:, block(j)], m_d_scales[:, block(j)], a_d_codes, a_d_scales)
-                nc.scalar.copy(out=in_runs(db[j]), in_=by_slot(bank))
+        def grad_b(j):
+            quantize(m_d_codes[j], m_d_scales[j], m_weave[:, block(j, E)], E5M2)
+            product(db_ps[j], m_d_codes[j], m_d_scales[j], E5M2, a_d_codes, a_d_scales)
 
-        def stage_half(t, half):
-            nc.scalar.copy(out=in_runs(staged_half[t][half]), in_=by_slot(grad_ps[t % 2])[:, block(half, N // 64)])
+        def scatter(move, window, values, part):
+            move(windows[window].indirect(part_of_list(part, 2)), values[:, block(part, N // 2)])
 
-        def scatter_half(t, half):
-            nc.vector.tensor_copy(windows[t][:].indirect(offsets[:, block(half, N // 32)]), staged_half[t][half])
-            if half == 1:
-                nc.sync.dma_start(out=da_rows[t], in_=windows[t][:])
-
-        def scatter(out_rows, values, t):
-            nc.vector.tensor_copy(windows[t][:].indirect(offsets[:]), values[t])
-            nc.sync.dma_start(out=out_rows[t], in_=windows[t][:])
+        def store(target, window):
+            nc.sync.dma_start(out=target, in_=windows[window])
 
         for s in range(PACK):
-            nc.tensor.transpose(cb_ps[:, block(s)], cb_col[:, s : s + 1].to_broadcast([P, P]), ident[:])
-        nc.scalar.copy(out=in_fours(cb_row[:]), in_=by_e(cb_ps))
-        nc.scalar.activation(out=scale2[:], in_=cb_row[:], func=COPY, scale=ca_col[:, 2:3])
-
-        def turn_b(s):
-            turn(word_runs(b_got[:, block(s, N)]), b_turn[s], turn_ps[(s + 1) % 2])
-            quantize(b_i_codes[:, block(s)], b_i_scales[:, block(s)], b_turn[s], E4M3)
+            nc.tensor.transpose(cb_ps[:, block(s)], cb_col[:, s : s + 1].to_broadcast([P, P]), ident)
+        scalar_copy(in_fours(cb_row), by_e(cb_ps))
+        for t in range(1, PACK):
+            nc.scalar.activation(out=scale[t], in_=cb_row, func=COPY, scale=ca_col[:, t : t + 1])
 
         for s in range(PACK):
-            gather(b_got, b_raw, s)
+            gather(vector_copy, b_got[s], b_raw[s])
+            turn(b_got[s], turn_ps[s % 2])
+            if s == PACK - 1:
+                weave(scalar_copy, b_weave, b_planes, 2, 4)
+                weave(vector_copy, b_weave, b_planes, 3, 4)
+                weave(vector_copy, b_weave, b_planes, 0, 2)
+            turned(scalar_copy, b_turn[s], turn_ps[s % 2])
             if s < PACK - 1:
-                turn_b(s)
-        weave(nc.vector.tensor_copy, b_weave, b_got, 3, 4)
-        for part in range(3):
-            weave(nc.scalar.copy, b_weave, b_got, part, 4)
+                quantize(b_i_codes[:, block(s)], b_i_scales[:, block(s)], b_turn[s], E4M3)
 
-        da_rows, db_rows = rows(out_0), out_1.rearrange("(j q) n -> j q n", q=P)
-        gather(a_got, a_raw, 0)
-        weight[0], b_turn[3] = got[:, 0 : 2 * N].bitcast(F32), sb("b_turn3", N, BF16, tag="a_raw0")[:]
-        form_weight(0)
-        turn_b(3)
-        b_e_codes = sb("b_e_codes", N, U32, tag="wm_raw0")
-        quantize(b_e_codes[:], b_e_scales[:], b_weave, E4M3)
-        turn_a(0)
+        gather(vector_copy, a_got[0], a_raw[0], SPLIT, N)
+        gather(scalar_move, a_got[0], a_raw[0], 0, SPLIT)
+        quantize(b_i_codes[:, block(3)], b_i_scales[:, block(3)], b_turn[3], E4M3)
+        turn_a(0, scalar_copy)
+        weight[0] = sb("weight0", E, F32, tag="b_turn3")
+        weight_on_vector(0)
         correlate(0)
-        gather(a_got, a_raw, 1)
-        residual[0] = sb("residual0", E, F32)[:]
+        quantize(b_e_codes, b_e_scales, b_weave, E4M3)
+        gather(scalar_move, a_got[1], a_raw[1])
         scale_c(0, 2)
-        turn_a(1)
-        finish_m(0, nc.vector, 2, residual[0])
-        turn_m(0)
+        subtract(0, nc.vector, 2)
+        weigh(0, nc.vector, 2)
+        turn_m(0, scalar_copy)
+        turn_a(1, scalar_copy)
+        a_i_codes[1] = sb("a_i_codes1", P, U32, tag="b_turn3")
         correlate(1)
-        after_a1 = sb("after_a1", 2 * E, F32, tag="a_turn1")
-        weight[1], weight[2] = after_a1[:, 0:E], after_a1[:, E : 2 * E]
-        nc.gpsimd.tensor_tensor(out=weight[2], in0=wm_raw[2][:], in1=scale2[:], op=MULT)
-        gather(a_got, a_raw, 2)
-        residual[1] = sb("residual1", E, F32, tag="a_raw2")[:]
-        form_weight(1)
-        turn_a(2)
-        scale_c(1, 1)
-        m_e_codes[0] = sb("m_e_codes0", P, U32, tag="wm_raw1")
+        gather(vector_copy, a_got[2], a_raw[2])
+        weight[1] = sb("weight1", E, F32, tag="a_turn1")
+        weight_on_gpsimd(1)
+        m_e_codes[0] = sb("m_e_codes0", P, U32, tag="a_raw2")
         grad_a(0)
+        turn_a(2, scalar_copy)
+        scalar_copy(da[0], grad_ps[0])
+        scale_c(1, 2)
+        subtract(1, nc.vector, 2)
+        weigh(1, nc.vector, 2)
+        a_i_codes[2] = sb("a_i_codes2", P, U32, tag="tg_raw1")
         correlate(2)
-        finish_m(1, nc.gpsimd, 1, sb("difference1", E, F32, tag="a_turn2")[:])
-        gather(a_got, a_raw, 3)
-        after_a3 = sb("after_a3", N // 2 + 2 * E, F32, tag="a_raw3")
-        residual[2], weight[3] = after_a3[:, 0:E], after_a3[:, E : 2 * E]
-        staged_half[0] = [after_a3[:, 2 * E : 2 * E + N // 2], sb("staged0b", N // 2, F32)[:]]
-        staged_half[1] = [sb("staged1" + half, N // 2, F32)[:] for half in "ab"]
+        gather(vector_copy, a_got[3], a_raw[3])
+        weight[2] = sb("weight2", E, F32, tag="a_turn1")
+        weight_on_gpsimd(2)
+        weight[3] = sb("weight3", E, F32, tag="wm_raw2")
+        weight_on_gpsimd(3)
+        for part in range(2):
+            scatter(scalar_move, 0, da[0], part)
+        store(da_rows[0], 0)
+        after_a3 = sb("after_a3", E + E // 2, F32, tag="a_raw3")
+        residual[2], m_e[1] = after_a3[:, 0:E], after_a3[:, E:].bitcast(BF16)
+        turn_m(1, vector_copy)
         scale_c(2, 1)
-        form_weight(3)
-        stage_half(0, 0)
-        turn_a(3)
-        scatter_half(0, 0)
-        m_e[1] = sb("m_e1", E, BF16)[:]
-        turn_m(1)
-        stage_half(0, 1)
-        nc.gpsimd.tensor_tensor(out=residual[2], in0=residual[2], in1=tg_raw[2], op=SUBTRACT)
-        a_i_codes[3] = sb("a_i_codes3", P, U32, tag="tg_raw2")
-        correlate(3)
         grad_a(1)
-        nc.gpsimd.tensor_tensor(out=m_rows[:, block(2, E)], in0=residual[2], in1=weight[2], op=MULT)
-        scatter_half(0, 1)
-        scale_c(3, 1)
-        stage_half(1, 0)
-        for part in range(PACK):
-            weave(nc.scalar.copy, a_weave, a_got, part, PACK)
-        turn_m(2)
-        stage_half(1, 1)
-        a_d_codes = sb("a_d_codes", N, U32, tag="a_turn1")
-        quantize(a_d_codes[:], a_d_scales[:], a_weave, E4M3)
-        scatter_half(1, 0)
+        turn_a(3, vector_copy)
+        subtract(2, nc.vector, 1)
+        correlate(3)
+        weigh(2, nc.vector, 1)
+        weave(scalar_copy, a_weave, a_planes, 0, 4)
+        weave(vector_copy, a_weave, a_planes, 1, 2)
+        weave(vector_copy, a_weave, a_planes, 1, 4)
+        scalar_copy(da[1], grad_ps[1])
+        scale_c(3, 2)
+        subtract(3, nc.vector, 2)
+        turn_m(2, vector_copy)
+        weigh(3, nc.vector, 2)
+        for part in range(2):
+            scatter(scalar_move, 1, da[1], part)
+        store(da_rows[1], 1)
         grad_a(2)
-        finish_m(3, nc.gpsimd, 1, residual[3])
-        scatter_half(1, 1)
-        staged_half[2] = [sb("staged2a", N // 2, F32)[:], sb("staged2b", N // 2, F32)[:]]
-        stage_half(2, 0)
-        scatter_half(2, 0)
-        weave(nc.scalar.copy, m_weave, m_rows[:], 0, PACK)
-        turn_m(3)
-        grad_a(3)
-        stage_half(2, 1)
-        scatter_half(2, 1)
-        weave(nc.scalar.copy, m_weave, m_rows[:], 1, PACK)
-        stage_a(3)
-        weave(nc.scalar.copy, m_weave, m_rows[:], 1, 2)
+        weave(vector_copy, m_weave, m_planes, 0, 4)
+        quantize(a_d_codes, a_d_scales, a_weave, E4M3)
         grad_b(0)
-        scatter(da_rows, staged, 3)
+        weave(vector_copy, m_weave, m_planes, 1, 4)
+        turn_m(3, vector_copy)
         grad_b(1)
-        for j in range(PACK):
-            scatter(db_rows, db, j)
+        weave(vector_copy, m_weave, m_planes, 1, 2)
+        grad_a(3)
+        grad_b(2)
+        grad_b(3)
+        scalar_copy(da[2], grad_ps[2])
+        vector_copy(db[0], db_ps[0])
+        for part in range(2):
+            scatter(scalar_move, 2, da[2], part)
+        store(da_rows[2], 2)
+        for part in range(2):
+            scatter(vector_copy, 3, db[0], part)
+        store(db_rows[0], 3)
+        scalar_copy(db[1], db_ps[1])
+        vector_copy(da[3], grad_ps[0])
+        for part in range(2):
+            scatter(scalar_move, 4, db[1], part)
+        store(db_rows[1], 4)
+        for part in range(2):
+            scatter(vector_copy, 0, da[3], part)
+        store(da_rows[3], 0)
+        scalar_copy(db[2], db_ps[2])
+        vector_copy(db[3], db_ps[3])
+        for part in range(2):
+            scatter(scalar_move, 1, db[2], part)
+        store(db_rows[2], 1)
+        for part in range(2):
+            scatter(vector_copy, 2, db[3], part)
+        store(db_rows[3], 2)

@@ -52,27 +52,27 @@ def tile_attend_gbarlow_ab_kernel(tc, aT, bT, tg, wm, ca, cb, offs, out_0, out_1
         ca_col, cb_col = sb("ca_col", PACK, F32), sb("cb_col", PACK, F32)
         cb_row = sb("cb_row", E, F32)
         scale = {t: sb("scale" + str(t), E, F32) for t in range(1, PACK)}
-        a_start = PACK * N - N // 2
+        a_start = PACK * N
         got = sb("got", a_start + PACK * 2 * N, BF16)
         b_planes = got[:, 0 : PACK * N].rearrange("p (t x) -> p t x", t=PACK)
         a_planes = got[:, a_start:].rearrange("p (t x) -> p t x", t=PACK)[:, :, 0:N]
         b_got = [got[:, block(s, N)] for s in range(PACK)]
         a_got = [got[:, a_start:][:, block(2 * t, N)] for t in range(PACK)]
-        b_turn = planes("b_turn", N, BF16)
-        a_i_codes = {t: sb("a_i_codes" + str(t), P, U32) for t in (0, 3)}
+        b_turn = [sb("b_turn0", N, BF16), b_got[3], sb("b_turn2", N, BF16), sb("b_turn3", N, BF16)]
+        a_i_codes = {t: sb("a_i_codes" + str(t), P, U32) for t in (0, 2, 3)}
         a_i_scales = planes("a_i_scales", P, U8)
         b_i_codes, b_i_scales = sb("b_i_codes", E, U32), sb("b_i_scales", E, U8)
         a_weave, b_weave = sb("a_weave", PACK * N, BF16), sb("b_weave", PACK * N, BF16)
         a_d_codes, a_d_scales = sb("a_d_codes", N, U32), sb("a_d_scales", N, U8)
-        b_e_codes, b_e_scales = sb("b_e_codes", N, U32), sb("b_e_scales", N, U8)
-        a_turn = [a_got[1], sb("a_turn1", N, BF16), sb("a_turn2", N, BF16), a_weave[:, N + N // 2 : 2 * N + N // 2]]
+        b_e_scales = sb("b_e_scales", N, U8)
+        a_turn = [sb("a_turn0", N, BF16), sb("a_turn1", N, BF16), sb("a_turn2", N, BF16), a_weave[:, N + N // 2 : 2 * N + N // 2]]
         weight = {}
-        residual = {t: got[:, a_start:][:, block(t + 2, 2 * N)].bitcast(F32) for t in range(2)}
+        residual = {0: sb("residual0", E, F32), 1: got[:, a_start:][:, block(3, 2 * N)].bitcast(F32)}
         residual[3] = sb("residual3", E, F32)
         m_rows = sb("m_rows", PACK * E, BF16)
         m_planes = m_rows.rearrange("p (t x) -> p t x", t=PACK)
         m_e = {t: sb("m_e" + str(t), E, BF16) for t in (0, 2, 3)}
-        m_e_codes = {t: sb("m_e_codes" + str(t), P, U32) for t in range(1, PACK)}
+        m_e_codes = planes("m_e_codes", P, U32)
         m_e_scales = planes("m_e_scales", P, U8)
         m_weave = sb("m_weave", PACK * E, BF16)
         m_d_codes, m_d_scales = planes("m_d_codes", P, U32), planes("m_d_scales", P, U8)
@@ -97,15 +97,15 @@ def tile_attend_gbarlow_ab_kernel(tc, aT, bT, tg, wm, ca, cb, offs, out_0, out_1
         load(b_raw[0], b_rows[0])
         nc.sync.dma_start(offsets[:], offs)
         nc.scalar.dma_start(out=cb_col, in_=cb[0:1, :].rearrange("o (q s) -> q (o s)", s=PACK))
-        load(b_raw[1], b_rows[1])
-        nc.scalar.dma_start(out=ca_col, in_=ca.rearrange("(p t) o -> p (t o)", t=PACK))
-        load(b_raw[2], b_rows[2])
-        load(b_raw[3], b_rows[3])
         load(a_raw[0], a_rows[0])
-        load_w(0)
+        nc.scalar.dma_start(out=ca_col, in_=ca.rearrange("(p t) o -> p (t o)", t=PACK))
+        for s in range(1, PACK):
+            load(b_raw[s], b_rows[s])
         load(a_raw[1], a_rows[1])
+        load_w(0)
+        load(wm_raw[1], wm_rows[1])
         load(a_raw[2], a_rows[2])
-        load_w(1)
+        load(tg_raw[1], tg_rows[1])
         load(a_raw[3], a_rows[3])
         load_w(2)
         load_w(3)
@@ -166,9 +166,9 @@ def tile_attend_gbarlow_ab_kernel(tc, aT, bT, tg, wm, ca, cb, offs, out_0, out_1
         def in_fours(x):
             return x.rearrange("p (q s) -> p q s", s=PACK)
 
-        def turn_a(t, copy):
-            turn(a_got[t], turn_ps[t % 2])
-            turned(copy, a_turn[t], turn_ps[t % 2])
+        def turn_a(t, copy, into):
+            turn(a_got[t], into)
+            turned(copy, a_turn[t], into)
 
         def correlate(t):
             quantize(a_i_codes[t], a_i_scales[t], a_turn[t], E4M3)
@@ -199,8 +199,8 @@ def tile_attend_gbarlow_ab_kernel(tc, aT, bT, tg, wm, ca, cb, offs, out_0, out_1
                     op1=MULT,
                 )
 
-        def subtract(t, engine, parts):
-            for part in range(parts):
+        def subtract(t, engine, parts, which=None):
+            for part in which or range(parts):
                 cols = block(part, E // parts)
                 engine.tensor_tensor(
                     out=residual[t][:, cols], in0=residual[t][:, cols], in1=tg_raw[t][:, cols], op=SUBTRACT
@@ -230,6 +230,9 @@ def tile_attend_gbarlow_ab_kernel(tc, aT, bT, tg, wm, ca, cb, offs, out_0, out_1
         def scatter(move, window, values, part):
             move(windows[window].indirect(part_of_list(part, 2)), values[:, block(part, N // 2)])
 
+        def scatter_whole(window, values):
+            vector_copy(windows[window].indirect(offsets[:]), values)
+
         def store(target, window):
             nc.sync.dma_start(out=target, in_=windows[window])
 
@@ -239,47 +242,94 @@ def tile_attend_gbarlow_ab_kernel(tc, aT, bT, tg, wm, ca, cb, offs, out_0, out_1
         for t in range(1, PACK):
             nc.scalar.activation(out=scale[t], in_=cb_row, func=COPY, scale=ca_col[:, t : t + 1])
 
-        for s in range(PACK):
-            gather(vector_copy, b_got[s], b_raw[s])
-            turn(b_got[s], turn_ps[s % 2])
-            if s == PACK - 1:
-                weave(scalar_copy, b_weave, b_planes, 2, 4)
-                weave(vector_copy, b_weave, b_planes, 3, 4)
-                weave(vector_copy, b_weave, b_planes, 0, 2)
-            turned(scalar_copy, b_turn[s], turn_ps[s % 2])
-            if s < PACK - 1:
-                quantize(b_i_codes[:, block(s)], b_i_scales[:, block(s)], b_turn[s], E4M3)
+        def b_plane(s, copy):
+            into = turn_ps[(0, 0, 1, 0)[s]]
+            turn(b_got[s], into)
+            turned(copy, b_turn[s], into)
 
-        gather(vector_copy, a_got[0], a_raw[0], SPLIT, N)
-        gather(scalar_move, a_got[0], a_raw[0], 0, SPLIT)
-        quantize(b_i_codes[:, block(3)], b_i_scales[:, block(3)], b_turn[3], E4M3)
-        turn_a(0, scalar_copy)
+        def quantize_b(s):
+            quantize(b_i_codes[:, block(s)], b_i_scales[:, block(s)], b_turn[s], E4M3)
+
+        def correlate_first(into, cols):
+            product(into, a_i_codes[0], a_i_scales[0], E4M3, b_i_codes[:, cols], b_i_scales[:, cols])
+
+        def pairs(x, u):
+            return x.rearrange("p (q u v) -> p u q v", u=2, v=2)[:, u]
+
+        def half(x, u):
+            return x[:, block(u, E // 2)].rearrange("p (q v) -> p q v", v=2)
+
+        def scale_first(u):
+            nc.vector.scalar_tensor_tensor(
+                out=half(residual[0], u),
+                in0=c_ps[u][:, 0 : 2 * P].rearrange("p (v q) -> p q v", v=2),
+                scalar=ca_col[:, 0:1],
+                in1=pairs(cb_row, u),
+                op0=MULT,
+                op1=MULT,
+            )
+
+        def subtract_first(u):
+            nc.vector.tensor_tensor(
+                out=half(difference, u), in0=half(residual[0], u), in1=pairs(tg_raw[0], u), op=SUBTRACT
+            )
+
+        def weigh_first(u):
+            nc.vector.tensor_tensor(
+                out=pairs(m_rows[:, block(0, E)], u), in0=half(difference, u), in1=pairs(weight[0], u), op=MULT
+            )
+
+        gather(vector_copy, b_got[0], b_raw[0])
+        b_plane(0, scalar_copy)
+        quantize_b(0)
+        gather(vector_copy, a_got[0], a_raw[0])
+        turn(a_got[0], turn_ps[1])
+        turned(scalar_copy, a_turn[0], turn_ps[1])
+        quantize(a_i_codes[0], a_i_scales[0], a_turn[0], E4M3)
+        for s in (1, 2):
+            gather(vector_copy, b_got[s], b_raw[s])
+            b_plane(s, scalar_copy)
+            quantize_b(s)
+            if s == 1:
+                correlate_first(c_ps[0][:, 0 : 2 * P], slice(0, 2 * P))
+                scale_first(0)
+            else:
+                correlate_first(c_ps[1][:, block(0)], block(2))
+        gather(vector_copy, b_got[3], b_raw[3], SPLIT, N)
+        gather(scalar_move, b_got[3], b_raw[3], 0, SPLIT)
+        weave(scalar_copy, b_weave, b_planes, 0, 4)
+        b_plane(3, scalar_copy)
+        weave(vector_copy, b_weave, b_planes, 1, 2)
+        weave(vector_copy, b_weave, b_planes, 1, 4)
+        quantize_b(3)
+        correlate_first(c_ps[1][:, block(1)], block(3))
         weight[0] = sb("weight0", E, F32, tag="b_turn3")
         weight_on_vector(0)
-        correlate(0)
-        quantize(b_e_codes, b_e_scales, b_weave, E4M3)
         gather(scalar_move, a_got[1], a_raw[1])
-        scale_c(0, 2)
-        subtract(0, nc.vector, 2)
-        weigh(0, nc.vector, 2)
-        turn_m(0, scalar_copy)
-        turn_a(1, scalar_copy)
+        scale_first(1)
+        turn_a(1, scalar_copy, c_ps[1])
+        difference = sb("difference", E, F32, tag="wm_raw0")
+        for u in range(2):
+            subtract_first(u)
+        for u in range(2):
+            weigh_first(u)
         a_i_codes[1] = sb("a_i_codes1", P, U32, tag="b_turn3")
         correlate(1)
-        gather(vector_copy, a_got[2], a_raw[2])
-        weight[1] = sb("weight1", E, F32, tag="a_turn1")
+        b_e_codes = sb("b_e_codes", N, U32, tag="wm_raw0")
+        quantize(b_e_codes, b_e_scales, b_weave, E4M3)
+        weight[1] = sb("weight1", E, F32, tag="b_weave")
         weight_on_gpsimd(1)
-        m_e_codes[0] = sb("m_e_codes0", P, U32, tag="a_raw2")
-        grad_a(0)
-        turn_a(2, scalar_copy)
-        scalar_copy(da[0], grad_ps[0])
+        gather(scalar_move, a_got[2], a_raw[2])
+        turn_m(0, vector_copy)
         scale_c(1, 2)
+        grad_a(0)
         subtract(1, nc.vector, 2)
         weigh(1, nc.vector, 2)
-        a_i_codes[2] = sb("a_i_codes2", P, U32, tag="tg_raw1")
-        correlate(2)
+        scalar_copy(da[0], grad_ps[0])
+        turn_a(2, scalar_copy, c_ps[1])
         gather(vector_copy, a_got[3], a_raw[3])
-        weight[2] = sb("weight2", E, F32, tag="a_turn1")
+        correlate(2)
+        weight[2] = sb("weight2", E, F32, tag="wm_raw1")
         weight_on_gpsimd(2)
         weight[3] = sb("weight3", E, F32, tag="wm_raw2")
         weight_on_gpsimd(3)
@@ -290,23 +340,23 @@ def tile_attend_gbarlow_ab_kernel(tc, aT, bT, tg, wm, ca, cb, offs, out_0, out_1
         residual[2], m_e[1] = after_a3[:, 0:E], after_a3[:, E:].bitcast(BF16)
         turn_m(1, vector_copy)
         scale_c(2, 1)
+        turn_a(3, vector_copy, turn_ps[1])
         grad_a(1)
-        turn_a(3, vector_copy)
         subtract(2, nc.vector, 1)
         correlate(3)
         weigh(2, nc.vector, 1)
         weave(scalar_copy, a_weave, a_planes, 0, 4)
         weave(vector_copy, a_weave, a_planes, 1, 2)
-        weave(vector_copy, a_weave, a_planes, 1, 4)
         scalar_copy(da[1], grad_ps[1])
-        scale_c(3, 2)
-        subtract(3, nc.vector, 2)
         turn_m(2, vector_copy)
+        scale_c(3, 2)
+        grad_a(2)
+        subtract(3, nc.vector, 2)
         weigh(3, nc.vector, 2)
         for part in range(2):
             scatter(scalar_move, 1, da[1], part)
         store(da_rows[1], 1)
-        grad_a(2)
+        weave(vector_copy, a_weave, a_planes, 1, 4)
         weave(vector_copy, m_weave, m_planes, 0, 4)
         quantize(a_d_codes, a_d_scales, a_weave, E4M3)
         grad_b(0)
@@ -322,22 +372,19 @@ def tile_attend_gbarlow_ab_kernel(tc, aT, bT, tg, wm, ca, cb, offs, out_0, out_1
         for part in range(2):
             scatter(scalar_move, 2, da[2], part)
         store(da_rows[2], 2)
-        for part in range(2):
-            scatter(vector_copy, 3, db[0], part)
+        scatter_whole(3, db[0])
         store(db_rows[0], 3)
         scalar_copy(db[1], db_ps[1])
         vector_copy(da[3], grad_ps[0])
         for part in range(2):
             scatter(scalar_move, 4, db[1], part)
         store(db_rows[1], 4)
-        for part in range(2):
-            scatter(vector_copy, 0, da[3], part)
+        scatter_whole(0, da[3])
         store(da_rows[3], 0)
-        scalar_copy(db[2], db_ps[2])
+        vector_copy(db[2], db_ps[2])
         vector_copy(db[3], db_ps[3])
         for part in range(2):
             scatter(scalar_move, 1, db[2], part)
         store(db_rows[2], 1)
-        for part in range(2):
-            scatter(vector_copy, 2, db[3], part)
+        scatter_whole(2, db[3])
         store(db_rows[3], 2)

@@ -103,9 +103,8 @@ def tile_attend_gbarlow_ab_kernel(tc, aT, bT, tg, wm, ca, cb, offs, out_0, out_1
             load(b_raw[s], b_rows[s])
         load(a_raw[1], a_rows[1])
         load_w(0)
-        load(wm_raw[1], wm_rows[1])
         load(a_raw[2], a_rows[2])
-        load(tg_raw[1], tg_rows[1])
+        load_w(1)
         load(a_raw[3], a_rows[3])
         load_w(2)
         load_w(3)
@@ -187,8 +186,8 @@ def tile_attend_gbarlow_ab_kernel(tc, aT, bT, tg, wm, ca, cb, offs, out_0, out_1
         def weight_on_gpsimd(t):
             nc.gpsimd.tensor_tensor(out=weight[t], in0=wm_raw[t], in1=scale[t], op=MULT)
 
-        def scale_c(t, parts):
-            for part in range(parts):
+        def scale_c(t, parts, which=None):
+            for part in which or range(parts):
                 cols = block(part, E // parts)
                 nc.vector.scalar_tensor_tensor(
                     out=in_fours(residual[t][:, cols]),
@@ -232,6 +231,10 @@ def tile_attend_gbarlow_ab_kernel(tc, aT, bT, tg, wm, ca, cb, offs, out_0, out_1
 
         def scatter_whole(window, values):
             vector_copy(windows[window].indirect(offsets[:]), values)
+
+        def stage(values, source):
+            for part in range(2):
+                scalar_copy(values[:, block(part, N // 2)], source[:, block(part, N // 2)])
 
         def store(target, window):
             nc.sync.dma_start(out=target, in_=windows[window])
@@ -321,12 +324,13 @@ def tile_attend_gbarlow_ab_kernel(tc, aT, bT, tg, wm, ca, cb, offs, out_0, out_1
         weight_on_gpsimd(1)
         gather(scalar_move, a_got[2], a_raw[2])
         turn_m(0, vector_copy)
-        scale_c(1, 2)
+        turn_a(2, scalar_copy, turn_ps[0])
+        scale_c(1, 2, (0,))
         grad_a(0)
+        scale_c(1, 2, (1,))
         subtract(1, nc.vector, 2)
         weigh(1, nc.vector, 2)
-        scalar_copy(da[0], grad_ps[0])
-        turn_a(2, scalar_copy, c_ps[1])
+        stage(da[0], grad_ps[0])
         gather(vector_copy, a_got[3], a_raw[3])
         correlate(2)
         weight[2] = sb("weight2", E, F32, tag="wm_raw1")
@@ -345,18 +349,18 @@ def tile_attend_gbarlow_ab_kernel(tc, aT, bT, tg, wm, ca, cb, offs, out_0, out_1
         subtract(2, nc.vector, 1)
         correlate(3)
         weigh(2, nc.vector, 1)
-        weave(scalar_copy, a_weave, a_planes, 0, 4)
         weave(vector_copy, a_weave, a_planes, 1, 2)
-        scalar_copy(da[1], grad_ps[1])
+        stage(da[1], grad_ps[1])
         turn_m(2, vector_copy)
-        scale_c(3, 2)
+        scale_c(3, 2, (0,))
         grad_a(2)
+        scale_c(3, 2, (1,))
         subtract(3, nc.vector, 2)
         weigh(3, nc.vector, 2)
         for part in range(2):
             scatter(scalar_move, 1, da[1], part)
         store(da_rows[1], 1)
-        weave(vector_copy, a_weave, a_planes, 1, 4)
+        weave(vector_copy, a_weave, a_planes, 0, 2)
         weave(vector_copy, m_weave, m_planes, 0, 4)
         quantize(a_d_codes, a_d_scales, a_weave, E4M3)
         grad_b(0)
@@ -367,21 +371,22 @@ def tile_attend_gbarlow_ab_kernel(tc, aT, bT, tg, wm, ca, cb, offs, out_0, out_1
         grad_a(3)
         grad_b(2)
         grad_b(3)
-        scalar_copy(da[2], grad_ps[2])
+        stage(da[2], grad_ps[2])
         vector_copy(db[0], db_ps[0])
         for part in range(2):
             scatter(scalar_move, 2, da[2], part)
         store(da_rows[2], 2)
         scatter_whole(3, db[0])
         store(db_rows[0], 3)
-        scalar_copy(db[1], db_ps[1])
+        stage(db[1], db_ps[1])
         vector_copy(da[3], grad_ps[0])
         for part in range(2):
             scatter(scalar_move, 4, db[1], part)
         store(db_rows[1], 4)
         scatter_whole(0, da[3])
         store(da_rows[3], 0)
-        vector_copy(db[2], db_ps[2])
+        scalar_copy(db[2][:, block(0, N // 2)], db_ps[2][:, block(0, N // 2)])
+        scalar_copy(db[2][:, block(1, N // 2)], db_ps[2][:, block(1, N // 2)])
         vector_copy(db[3], db_ps[3])
         for part in range(2):
             scatter(scalar_move, 1, db[2], part)

@@ -21,7 +21,7 @@ SUBTRACT = mybir.AluOpType.subtract
 P = 128
 PACK = 4
 WINDOWS = 5
-SPLIT = 192
+SPLIT = 256
 
 
 def tile_attend_gbarlow_ab_kernel(tc, aT, bT, tg, wm, ca, cb, offs, out_0, out_1):
@@ -64,7 +64,7 @@ def tile_attend_gbarlow_ab_kernel(tc, aT, bT, tg, wm, ca, cb, offs, out_0, out_1
         b_i_codes, b_i_scales = sb("b_i_codes", E, U32), sb("b_i_scales", E, U8)
         a_weave, b_weave = sb("a_weave", PACK * N, BF16), sb("b_weave", PACK * N, BF16)
         a_d_codes, a_d_scales = sb("a_d_codes", N, U32), sb("a_d_scales", N, U8)
-        b_e_scales = sb("b_e_scales", N, U8)
+        b_e_codes, b_e_scales = sb("b_e_codes", N, U32), sb("b_e_scales", N, U8)
         a_turn = [sb("a_turn0", N, BF16), sb("a_turn1", N, BF16), sb("a_turn2", N, BF16), a_weave[:, N + N // 2 : 2 * N + N // 2]]
         weight = {}
         residual = {0: sb("residual0", E, F32), 1: got[:, a_start:][:, block(3, 2 * N)].bitcast(F32)}
@@ -304,6 +304,9 @@ def tile_attend_gbarlow_ab_kernel(tc, aT, bT, tg, wm, ca, cb, offs, out_0, out_1
         b_plane(3, scalar_copy)
         weave(vector_copy, b_weave, b_planes, 1, 2)
         weave(vector_copy, b_weave, b_planes, 1, 4)
+        for part in (1, 0):
+            cols = block(part, N // 2)
+            quantize(b_e_codes[:, cols], b_e_scales[:, cols], b_weave[:, block(part, 2 * N)], E4M3)
         quantize_b(3)
         correlate_first(c_ps[1][:, block(1)], block(3))
         weight[0] = sb("weight0", E, F32, tag="b_turn3")
@@ -318,9 +321,7 @@ def tile_attend_gbarlow_ab_kernel(tc, aT, bT, tg, wm, ca, cb, offs, out_0, out_1
             weigh_first(u)
         a_i_codes[1] = sb("a_i_codes1", P, U32, tag="b_turn3")
         correlate(1)
-        b_e_codes = sb("b_e_codes", N, U32, tag="wm_raw0")
-        quantize(b_e_codes, b_e_scales, b_weave, E4M3)
-        weight[1] = sb("weight1", E, F32, tag="b_weave")
+        weight[1] = sb("weight1", E, F32, tag="a_turn1")
         weight_on_gpsimd(1)
         gather(scalar_move, a_got[2], a_raw[2])
         turn_m(0, vector_copy)

@@ -75,7 +75,7 @@ def tile_attend_gbarlow_ab_kernel(tc, aT, bT, tg, wm, ca, cb, offs, out_0, out_1
         m_e_codes = planes("m_e_codes", P, U32)
         m_e_scales = planes("m_e_scales", P, U8)
         m_weave = sb("m_weave", PACK * E, BF16)
-        m_d_codes, m_d_scales = planes("m_d_codes", P, U32), planes("m_d_scales", P, U8)
+        m_d_codes, m_d_scales = planes("m_d_codes", 2 * P, U32, 2), planes("m_d_scales", 2 * P, U8, 2)
         da, db = planes("da", N, F32), planes("db", N, F32)
         windows = planes("window", T, F32, WINDOWS)
 
@@ -222,9 +222,11 @@ def tile_attend_gbarlow_ab_kernel(tc, aT, bT, tg, wm, ca, cb, offs, out_0, out_1
 
         db_ps = (turn_ps[0], c_ps[0], cb_ps, turn_ps[1])
 
-        def grad_b(j):
-            quantize(m_d_codes[j], m_d_scales[j], m_weave[:, block(j, E)], E5M2)
-            product(db_ps[j], m_d_codes[j], m_d_scales[j], E5M2, a_d_codes, a_d_scales)
+        def grad_b(part):
+            quantize(m_d_codes[part], m_d_scales[part], m_weave[:, block(part, 2 * E)], E5M2)
+            for j in range(2):
+                codes, scales = m_d_codes[part][:, block(j)], m_d_scales[part][:, block(j)]
+                product(db_ps[2 * part + j], codes, scales, E5M2, a_d_codes, a_d_scales)
 
         def scatter(move, window, values, part):
             move(windows[window].indirect(part_of_list(part, 2)), values[:, block(part, N // 2)])
@@ -309,17 +311,17 @@ def tile_attend_gbarlow_ab_kernel(tc, aT, bT, tg, wm, ca, cb, offs, out_0, out_1
             quantize(b_e_codes[:, cols], b_e_scales[:, cols], b_weave[:, block(part, 2 * N)], E4M3)
         quantize_b(3)
         correlate_first(c_ps[1][:, block(1)], block(3))
-        weight[0] = sb("weight0", E, F32, tag="b_turn3")
+        weight[0] = sb("weight0", E, F32, tag="b_weave")
         weight_on_vector(0)
         gather(scalar_move, a_got[1], a_raw[1])
         scale_first(1)
-        turn_a(1, scalar_copy, c_ps[1])
+        turn_a(1, scalar_copy, cb_ps)
         difference = sb("difference", E, F32, tag="wm_raw0")
         for u in range(2):
             subtract_first(u)
         for u in range(2):
             weigh_first(u)
-        a_i_codes[1] = sb("a_i_codes1", P, U32, tag="b_turn3")
+        a_i_codes[1] = sb("a_i_codes1", P, U32, tag="b_weave")
         correlate(1)
         weight[1] = sb("weight1", E, F32, tag="a_turn1")
         weight_on_gpsimd(1)
@@ -327,17 +329,21 @@ def tile_attend_gbarlow_ab_kernel(tc, aT, bT, tg, wm, ca, cb, offs, out_0, out_1
         turn_m(0, vector_copy)
         turn_a(2, scalar_copy, turn_ps[0])
         scale_c(1, 2, (0,))
-        grad_a(0)
+        quantize(m_e_codes[0], m_e_scales[0], m_e[0], E5M2)
+        first_ps = (grad_ps[0], turn_ps[1])
+        for part in range(2):
+            cols = block(part, N // 2)
+            product(first_ps[part][:, cols], m_e_codes[0], m_e_scales[0], E5M2, b_e_codes[:, cols], b_e_scales[:, cols])
         scale_c(1, 2, (1,))
         subtract(1, nc.vector, 2)
-        weigh(1, nc.vector, 2)
-        stage(da[0], grad_ps[0])
-        gather(vector_copy, a_got[3], a_raw[3])
         correlate(2)
+        weigh(1, nc.vector, 2)
+        for part in range(2):
+            cols = block(part, N // 2)
+            scalar_copy(da[0][:, cols], first_ps[part][:, cols])
+        gather(vector_copy, a_got[3], a_raw[3])
         weight[2] = sb("weight2", E, F32, tag="wm_raw1")
         weight_on_gpsimd(2)
-        weight[3] = sb("weight3", E, F32, tag="wm_raw2")
-        weight_on_gpsimd(3)
         for part in range(2):
             scatter(scalar_move, 0, da[0], part)
         store(da_rows[0], 0)
@@ -350,28 +356,27 @@ def tile_attend_gbarlow_ab_kernel(tc, aT, bT, tg, wm, ca, cb, offs, out_0, out_1
         subtract(2, nc.vector, 1)
         correlate(3)
         weigh(2, nc.vector, 1)
+        weight[3] = sb("weight3", E, F32, tag="wm_raw1")
+        weight_on_gpsimd(3)
+        weave(scalar_copy, a_weave, a_planes, 0, 4)
         weave(vector_copy, a_weave, a_planes, 1, 2)
         stage(da[1], grad_ps[1])
         turn_m(2, vector_copy)
-        scale_c(3, 2, (0,))
+        scale_c(3, 1)
         grad_a(2)
-        scale_c(3, 2, (1,))
         subtract(3, nc.vector, 2)
         weigh(3, nc.vector, 2)
         for part in range(2):
             scatter(scalar_move, 1, da[1], part)
         store(da_rows[1], 1)
-        weave(vector_copy, a_weave, a_planes, 0, 2)
-        weave(vector_copy, m_weave, m_planes, 0, 4)
+        weave(vector_copy, a_weave, a_planes, 1, 4)
+        weave(vector_copy, m_weave, m_planes, 0, 2)
         quantize(a_d_codes, a_d_scales, a_weave, E4M3)
         grad_b(0)
-        weave(vector_copy, m_weave, m_planes, 1, 4)
         turn_m(3, vector_copy)
-        grad_b(1)
         weave(vector_copy, m_weave, m_planes, 1, 2)
         grad_a(3)
-        grad_b(2)
-        grad_b(3)
+        grad_b(1)
         stage(da[2], grad_ps[2])
         vector_copy(db[0], db_ps[0])
         for part in range(2):

@@ -358,7 +358,6 @@ def tile_attend_gbarlow_ab_kernel(tc, aT, bT, tg, wm, ca, cb, offs, out_0, out_1
         weigh(2, nc.vector, 1)
         weight[3] = sb("weight3", E, F32, tag="wm_raw1")
         weight_on_gpsimd(3)
-        weave(scalar_copy, a_weave, a_planes, 0, 4)
         weave(vector_copy, a_weave, a_planes, 1, 2)
         stage(da[1], grad_ps[1])
         turn_m(2, vector_copy)
@@ -369,7 +368,7 @@ def tile_attend_gbarlow_ab_kernel(tc, aT, bT, tg, wm, ca, cb, offs, out_0, out_1
         for part in range(2):
             scatter(scalar_move, 1, da[1], part)
         store(da_rows[1], 1)
-        weave(vector_copy, a_weave, a_planes, 1, 4)
+        weave(vector_copy, a_weave, a_planes, 0, 2)
         weave(vector_copy, m_weave, m_planes, 0, 2)
         quantize(a_d_codes, a_d_scales, a_weave, E4M3)
         grad_b(0)

@@ -75,7 +75,7 @@ def tile_attend_gbarlow_ab_kernel(tc, aT, bT, tg, wm, ca, cb, offs, out_0, out_1
         m_e_codes = planes("m_e_codes", P, U32)
         m_e_scales = planes("m_e_scales", P, U8)
         m_weave = sb("m_weave", PACK * E, BF16)
-        m_d_codes, m_d_scales = planes("m_d_codes", 2 * P, U32, 2), planes("m_d_scales", 2 * P, U8, 2)
+        m_d_codes, m_d_scales = planes("m_d_codes", P, U32), planes("m_d_scales", P, U8)
         da, db = planes("da", N, F32), planes("db", N, F32)
         windows = planes("window", T, F32, WINDOWS)
 
@@ -222,11 +222,9 @@ def tile_attend_gbarlow_ab_kernel(tc, aT, bT, tg, wm, ca, cb, offs, out_0, out_1
 
         db_ps = (turn_ps[0], c_ps[0], cb_ps, turn_ps[1])
 
-        def grad_b(part):
-            quantize(m_d_codes[part], m_d_scales[part], m_weave[:, block(part, 2 * E)], E5M2)
-            for j in range(2):
-                codes, scales = m_d_codes[part][:, block(j)], m_d_scales[part][:, block(j)]
-                product(db_ps[2 * part + j], codes, scales, E5M2, a_d_codes, a_d_scales)
+        def grad_b(j):
+            quantize(m_d_codes[j], m_d_scales[j], m_weave[:, block(j, E)], E5M2)
+            product(db_ps[j], m_d_codes[j], m_d_scales[j], E5M2, a_d_codes, a_d_scales)
 
         def scatter(move, window, values, part):
             move(windows[window].indirect(part_of_list(part, 2)), values[:, block(part, N // 2)])
@@ -351,8 +349,8 @@ def tile_attend_gbarlow_ab_kernel(tc, aT, bT, tg, wm, ca, cb, offs, out_0, out_1
         residual[2], m_e[1] = after_a3[:, 0:E], after_a3[:, E:].bitcast(BF16)
         turn_m(1, vector_copy)
         scale_c(2, 1)
-        turn_a(3, vector_copy, turn_ps[1])
         grad_a(1)
+        turn_a(3, vector_copy, turn_ps[1])
         subtract(2, nc.vector, 1)
         correlate(3)
         weigh(2, nc.vector, 1)
@@ -363,35 +361,38 @@ def tile_attend_gbarlow_ab_kernel(tc, aT, bT, tg, wm, ca, cb, offs, out_0, out_1
         turn_m(2, vector_copy)
         scale_c(3, 1)
         grad_a(2)
+        weave(vector_copy, a_weave, a_planes, 0, 2)
         subtract(3, nc.vector, 2)
         weigh(3, nc.vector, 2)
         for part in range(2):
             scatter(scalar_move, 1, da[1], part)
         store(da_rows[1], 1)
-        weave(vector_copy, a_weave, a_planes, 0, 2)
-        weave(vector_copy, m_weave, m_planes, 0, 2)
+        weave(vector_copy, m_weave, m_planes, 0, 4)
         quantize(a_d_codes, a_d_scales, a_weave, E4M3)
         grad_b(0)
-        turn_m(3, vector_copy)
-        weave(vector_copy, m_weave, m_planes, 1, 2)
-        grad_a(3)
-        grad_b(1)
         stage(da[2], grad_ps[2])
-        vector_copy(db[0], db_ps[0])
         for part in range(2):
             scatter(scalar_move, 2, da[2], part)
         store(da_rows[2], 2)
+        weave(vector_copy, m_weave, m_planes, 1, 4)
+        turn_m(3, vector_copy)
+        grad_b(1)
+        weave(vector_copy, m_weave, m_planes, 2, 4)
+        grad_a(3)
+        vector_copy(db[0], db_ps[0])
+        grad_b(2)
         scatter_whole(3, db[0])
         store(db_rows[0], 3)
+        weave(vector_copy, m_weave, m_planes, 3, 4)
         stage(db[1], db_ps[1])
         vector_copy(da[3], grad_ps[0])
+        grad_b(3)
         for part in range(2):
             scatter(scalar_move, 4, db[1], part)
         store(db_rows[1], 4)
         scatter_whole(0, da[3])
         store(da_rows[3], 0)
-        scalar_copy(db[2][:, block(0, N // 2)], db_ps[2][:, block(0, N // 2)])
-        scalar_copy(db[2][:, block(1, N // 2)], db_ps[2][:, block(1, N // 2)])
+        stage(db[2], db_ps[2])
         vector_copy(db[3], db_ps[3])
         for part in range(2):
             scatter(scalar_move, 1, db[2], part)

@@ -22,6 +22,7 @@ P = 128
 PACK = 4
 WINDOWS = 5
 SPLIT = 256
+EARLY = 192
 
 
 def tile_attend_gbarlow_ab_kernel(tc, aT, bT, tg, wm, ca, cb, offs, out_0, out_1):
@@ -106,8 +107,9 @@ def tile_attend_gbarlow_ab_kernel(tc, aT, bT, tg, wm, ca, cb, offs, out_0, out_1
         load(a_raw[2], a_rows[2])
         load_w(1)
         load(a_raw[3], a_rows[3])
-        load_w(2)
-        load_w(3)
+        for tiles, sources in ((wm_raw, wm_rows), (tg_raw, tg_rows)):
+            for t in (2, 3):
+                load(tiles[t], sources[t])
 
         make_identity(nc, ident)
         for k in range(WINDOWS):
@@ -141,8 +143,9 @@ def tile_attend_gbarlow_ab_kernel(tc, aT, bT, tg, wm, ca, cb, offs, out_0, out_1
                 source.rearrange("j (u r) -> j r u", u=2)[:, 0:P],
             )
 
-        def weave(copy, woven, source, part, parts):
-            cols = block(part, N // PACK // parts)
+        def weave(copy, woven, source, part, parts, count=1):
+            width = N // PACK // parts
+            cols = slice(part * width, (part + count) * width)
             copy(
                 woven.rearrange("p (c i t) -> p c t i", i=4, t=PACK)[:, cols],
                 source.rearrange("p t (c i) -> p c t i", i=4)[:, cols],
@@ -183,8 +186,8 @@ def tile_attend_gbarlow_ab_kernel(tc, aT, bT, tg, wm, ca, cb, offs, out_0, out_1
                 op1=MULT,
             )
 
-        def weight_on_gpsimd(t):
-            nc.gpsimd.tensor_tensor(out=weight[t], in0=wm_raw[t], in1=scale[t], op=MULT)
+        def weight_on_gpsimd(t, into, cols=slice(0, E)):
+            nc.gpsimd.tensor_tensor(out=into, in0=wm_raw[t][:, cols], in1=scale[t][:, cols], op=MULT)
 
         def scale_c(t, parts, which=None):
             for part in which or range(parts):
@@ -322,7 +325,7 @@ def tile_attend_gbarlow_ab_kernel(tc, aT, bT, tg, wm, ca, cb, offs, out_0, out_1
         a_i_codes[1] = sb("a_i_codes1", P, U32, tag="b_weave")
         correlate(1)
         weight[1] = sb("weight1", E, F32, tag="a_turn1")
-        weight_on_gpsimd(1)
+        weight_on_gpsimd(1, weight[1])
         gather(scalar_move, a_got[2], a_raw[2])
         turn_m(0, vector_copy)
         turn_a(2, scalar_copy, turn_ps[0])
@@ -341,7 +344,10 @@ def tile_attend_gbarlow_ab_kernel(tc, aT, bT, tg, wm, ca, cb, offs, out_0, out_1
             scalar_copy(da[0][:, cols], first_ps[part][:, cols])
         gather(vector_copy, a_got[3], a_raw[3])
         weight[2] = sb("weight2", E, F32, tag="wm_raw1")
-        weight_on_gpsimd(2)
+        weight_on_gpsimd(2, weight[2])
+        last_cols = (slice(0, EARLY), slice(EARLY, E))
+        last_weight = [sb("weight3_first", EARLY, F32)]
+        weight_on_gpsimd(3, last_weight[0], last_cols[0])
         for part in range(2):
             scatter(scalar_move, 0, da[0], part)
         store(da_rows[0], 0)
@@ -354,16 +360,18 @@ def tile_attend_gbarlow_ab_kernel(tc, aT, bT, tg, wm, ca, cb, offs, out_0, out_1
         subtract(2, nc.vector, 1)
         correlate(3)
         weigh(2, nc.vector, 1)
-        weight[3] = sb("weight3", E, F32, tag="wm_raw1")
-        weight_on_gpsimd(3)
+        last_weight.append(sb("weight3_second", E - EARLY, F32, tag="wm_raw1"))
+        weight_on_gpsimd(3, last_weight[1], last_cols[1])
+        weave(scalar_copy, a_weave, a_planes, 0, 8)
         weave(vector_copy, a_weave, a_planes, 1, 2)
         stage(da[1], grad_ps[1])
         turn_m(2, vector_copy)
         scale_c(3, 1)
         grad_a(2)
-        weave(vector_copy, a_weave, a_planes, 0, 2)
+        weave(vector_copy, a_weave, a_planes, 1, 8, 3)
         subtract(3, nc.vector, 2)
-        weigh(3, nc.vector, 2)
+        for cols, factor in zip(last_cols, last_weight):
+            nc.vector.tensor_tensor(out=m_rows[:, block(3, E)][:, cols], in0=residual[3][:, cols], in1=factor, op=MULT)
         for part in range(2):
             scatter(scalar_move, 1, da[1], part)
         store(da_rows[1], 1)

@@ -186,8 +186,8 @@ def tile_attend_gbarlow_ab_kernel(tc, aT, bT, tg, wm, ca, cb, offs, out_0, out_1
                 op1=MULT,
             )
 
-        def weight_on_gpsimd(t, into, cols=slice(0, E)):
-            nc.gpsimd.tensor_tensor(out=into, in0=wm_raw[t][:, cols], in1=scale[t][:, cols], op=MULT)
+        def weight_on_gpsimd(t, cols=slice(0, E)):
+            nc.gpsimd.tensor_tensor(out=weight[t][:, cols], in0=wm_raw[t][:, cols], in1=scale[t][:, cols], op=MULT)
 
         def scale_c(t, parts, which=None):
             for part in which or range(parts):
@@ -325,7 +325,7 @@ def tile_attend_gbarlow_ab_kernel(tc, aT, bT, tg, wm, ca, cb, offs, out_0, out_1
         a_i_codes[1] = sb("a_i_codes1", P, U32, tag="b_weave")
         correlate(1)
         weight[1] = sb("weight1", E, F32, tag="a_turn1")
-        weight_on_gpsimd(1, weight[1])
+        weight_on_gpsimd(1)
         gather(scalar_move, a_got[2], a_raw[2])
         turn_m(0, vector_copy)
         turn_a(2, scalar_copy, turn_ps[0])
@@ -343,11 +343,10 @@ def tile_attend_gbarlow_ab_kernel(tc, aT, bT, tg, wm, ca, cb, offs, out_0, out_1
             cols = block(part, N // 2)
             scalar_copy(da[0][:, cols], first_ps[part][:, cols])
         gather(vector_copy, a_got[3], a_raw[3])
-        weight[2] = sb("weight2", E, F32, tag="wm_raw1")
-        weight_on_gpsimd(2, weight[2])
-        last_cols = (slice(0, EARLY), slice(EARLY, E))
-        last_weight = [sb("weight3_first", EARLY, F32)]
-        weight_on_gpsimd(3, last_weight[0], last_cols[0])
+        late_weights = sb("late_weights", EARLY + E, F32, tag="wm_raw1")
+        weight[2], weight[3] = late_weights[:, EARLY:], late_weights[:, 0:E]
+        weight_on_gpsimd(2)
+        weight_on_gpsimd(3, slice(0, EARLY))
         for part in range(2):
             scatter(scalar_move, 0, da[0], part)
         store(da_rows[0], 0)
@@ -360,8 +359,7 @@ def tile_attend_gbarlow_ab_kernel(tc, aT, bT, tg, wm, ca, cb, offs, out_0, out_1
         subtract(2, nc.vector, 1)
         correlate(3)
         weigh(2, nc.vector, 1)
-        last_weight.append(sb("weight3_second", E - EARLY, F32, tag="wm_raw1"))
-        weight_on_gpsimd(3, last_weight[1], last_cols[1])
+        weight_on_gpsimd(3, slice(EARLY, E))
         weave(scalar_copy, a_weave, a_planes, 0, 8)
         weave(vector_copy, a_weave, a_planes, 1, 2)
         stage(da[1], grad_ps[1])
@@ -370,8 +368,7 @@ def tile_attend_gbarlow_ab_kernel(tc, aT, bT, tg, wm, ca, cb, offs, out_0, out_1
         grad_a(2)
         weave(vector_copy, a_weave, a_planes, 1, 8, 3)
         subtract(3, nc.vector, 2)
-        for cols, factor in zip(last_cols, last_weight):
-            nc.vector.tensor_tensor(out=m_rows[:, block(3, E)][:, cols], in0=residual[3][:, cols], in1=factor, op=MULT)
+        weigh(3, nc.vector, 2)
         for part in range(2):
             scatter(scalar_move, 1, da[1], part)
         store(da_rows[1], 1)

from contextlib import ExitStack

import concourse.mybir as mybir
from concourse.masks import make_identity

D, E, T, N = 512, 512, 2048, 512
FLOPS = 3 * 2 * D * E * N

F32 = mybir.dt.float32
BF16 = mybir.dt.bfloat16
I32 = mybir.dt.int32
U32 = mybir.dt.uint32
U16 = mybir.dt.uint16
U8 = mybir.dt.uint8
E4M3 = mybir.dt.float8_e4m3fn_x4
E5M2 = mybir.dt.float8_e5m2_x4
COPY = mybir.ActivationFunctionType.Copy
MULT = mybir.AluOpType.mult
SUBTRACT = mybir.AluOpType.subtract

P = 128
PACK = 4
WINDOWS = 5
SPLIT = 256
EARLY = 192


def tile_attend_gbarlow_ab_kernel(tc, aT, bT, tg, wm, ca, cb, offs, out_0, out_1):
    nc = tc.nc
    with ExitStack() as ctx:
        keep = ctx.enter_context(tc.tile_pool(name="keep", bufs=1))
        psum = ctx.enter_context(tc.psum_pool(name="psum", bufs=1))

        def sb(name, width, dtype, tag=None):
            return keep.tile([P, width], dtype, name=name, tag=tag or name, align_bytes=256)[:]

        def planes(name, width, dtype, count=PACK):
            return [sb(name + str(t), width, dtype) for t in range(count)]

        def block(t, width=P):
            return slice(t * width, (t + 1) * width)

        def rows(x):
            return x.rearrange("(p t) n -> t p n", t=PACK)

        def bank(name):
            return psum.tile([P, 512], F32, name=name)[:]

        offsets = keep.tile([P, N // 16], U16, name="offsets")
        ident = sb("ident", P, F32)
        a_raw, b_raw = planes("a_raw", T, F32), planes("b_raw", T, F32)
        wm_raw, tg_raw = planes("wm_raw", E, F32), planes("tg_raw", E, F32)
        ca_col, cb_col = sb("ca_col", PACK, F32), sb("cb_col", PACK, F32)
        cb_row = sb("cb_row", E, F32)
        scale = {t: sb("scale" + str(t), E, F32) for t in range(1, PACK)}
        a_start = PACK * N
        got = sb("got", a_start + PACK * 2 * N, BF16)
        b_planes = got[:, 0 : PACK * N].rearrange("p (t x) -> p t x", t=PACK)
        a_planes = got[:, a_start:].rearrange("p (t x) -> p t x", t=PACK)[:, :, 0:N]
        b_got = [got[:, block(s, N)] for s in range(PACK)]
        a_got = [got[:, a_start:][:, block(2 * t, N)] for t in range(PACK)]
        b_turn = [sb("b_turn0", N, BF16), b_got[3], sb("b_turn2", N, BF16), sb("b_turn3", N, BF16)]
        a_i_codes = {t: sb("a_i_codes" + str(t), P, U32) for t in (0, 2, 3)}
        a_i_scales = planes("a_i_scales", P, U8)
        b_i_codes, b_i_scales = sb("b_i_codes", E, U32), sb("b_i_scales", E, U8)
        a_weave, b_weave = sb("a_weave", PACK * N, BF16), sb("b_weave", PACK * N, BF16)
        a_d_codes, a_d_scales = sb("a_d_codes", N, U32), sb("a_d_scales", N, U8)
        b_e_codes, b_e_scales = sb("b_e_codes", N, U32), sb("b_e_scales", N, U8)
        a_turn = [sb("a_turn0", N, BF16), sb("a_turn1", N, BF16), sb("a_turn2", N, BF16), a_weave[:, N + N // 2 : 2 * N + N // 2]]
        weight = {}
        residual = {0: sb("residual0", E, F32), 1: got[:, a_start:][:, block(3, 2 * N)].bitcast(F32)}
        residual[3] = sb("residual3", E, F32)
        m_rows = sb("m_rows", PACK * E, BF16)
        m_planes = m_rows.rearrange("p (t x) -> p t x", t=PACK)
        m_e = {t: sb("m_e" + str(t), E, BF16) for t in (0, 2, 3)}
        m_e_codes = planes("m_e_codes", P, U32)
        m_e_scales = planes("m_e_scales", P, U8)
        m_weave = sb("m_weave", PACK * E, BF16)
        m_d_codes, m_d_scales = planes("m_d_codes", P, U32), planes("m_d_scales", P, U8)
        da, db = planes("da", N, F32), planes("db", N, F32)
        windows = planes("window", T, F32, WINDOWS)

        cb_ps = bank("cb_ps")
        turn_ps = [bank("turn_ps0"), bank("turn_ps1")]
        c_ps = [bank("c_ps0"), bank("c_ps1")]
        grad_ps = [bank("grad_ps0"), bank("grad_ps1"), bank("grad_ps2")]

        a_rows, b_rows, wm_rows, tg_rows = rows(aT), rows(bT), rows(wm), rows(tg)
        da_rows, db_rows = rows(out_0), out_1.rearrange("(j q) n -> j q n", q=P)

        def load(tile, source):
            nc.sync.dma_start(out=tile, in_=source)

        def load_w(t):
            load(wm_raw[t], wm_rows[t])
            load(tg_raw[t], tg_rows[t])

        load(b_raw[0], b_rows[0])
        nc.sync.dma_start(offsets[:], offs)
        nc.scalar.dma_start(out=cb_col, in_=cb[0:1, :].rearrange("o (q s) -> q (o s)", s=PACK))
        load(a_raw[0], a_rows[0])
        nc.scalar.dma_start(out=ca_col, in_=ca.rearrange("(p t) o -> p (t o)", t=PACK))
        for s in range(1, PACK):
            load(b_raw[s], b_rows[s])
        load(a_raw[1], a_rows[1])
        load_w(0)
        load(a_raw[2], a_rows[2])
        load_w(1)
        load(a_raw[3], a_rows[3])
        for tiles, sources in ((wm_raw, wm_rows), (tg_raw, tg_rows)):
            for t in (2, 3):
                load(tiles[t], sources[t])

        make_identity(nc, ident)
        for k in range(WINDOWS):
            (nc.vector if k < 2 else nc.gpsimd).memset(windows[k].bitcast(I32), 0)

        def vector_copy(out, in_):
            nc.vector.tensor_copy(out, in_)

        def scalar_copy(out, in_):
            nc.scalar.copy(out=out, in_=in_)

        def scalar_move(out, in_):
            nc.scalar.activation(out, in_, COPY)

        def part_of_list(part, parts):
            return offsets[:, block(part, N // 16 // parts)]

        def quantize(codes, scales, values, fmt):
            nc.vector.quantize_mx(out=codes.bitcast(fmt), scales=scales, in_=values)

        def gather(move, target, raw, first=0, last=N):
            move(target[:, first:last], raw.indirect(offsets[:, first // 16 : last // 16]))

        def turn(source, into):
            for u in range(2):
                nc.tensor.transpose(into[:, block(2 * u)], source.bitcast(F32)[:, u : 2 * P : 2], ident)

        def turned(copy, target, source):
            copy(
                target.bitcast(F32).rearrange("j (r u) -> j r u", u=2),
                source.rearrange("j (u r) -> j r u", u=2)[:, 0:P],
            )

        def weave(copy, woven, source, part, parts, count=1):
            width = N // PACK // parts
            cols = slice(part * width, (part + count) * width)
            copy(
                woven.rearrange("p (c i t) -> p c t i", i=4, t=PACK)[:, cols],
                source.rearrange("p t (c i) -> p c t i", i=4)[:, cols],
            )

        def product(into, codes, scales, fmt, moving_codes, moving_scales):
            nc.tensor.matmul_mx(
                out=into,
                lhsT=codes.bitcast(fmt),
                lhsT_scale=scales,
                rhs=moving_codes.bitcast(E4M3),
                rhs_scale=moving_scales,
                start=True,
                stop=True,
            )

        def by_e(source):
            return source.rearrange("p (s q) -> p q s", s=PACK)

        def in_fours(x):
            return x.rearrange("p (q s) -> p q s", s=PACK)

        def turn_a(t, copy, into):
            turn(a_got[t], into)
            turned(copy, a_turn[t], into)

        def correlate(t):
            quantize(a_i_codes[t], a_i_scales[t], a_turn[t], E4M3)
            product(c_ps[t % 2], a_i_codes[t], a_i_scales[t], E4M3, b_i_codes, b_i_scales)

        def weight_on_vector(t):
            nc.vector.scalar_tensor_tensor(
                out=in_fours(weight[t]),
                in0=in_fours(wm_raw[t]),
                scalar=ca_col[:, t : t + 1],
                in1=by_e(cb_ps),
                op0=MULT,
                op1=MULT,
            )

        def weight_on_gpsimd(t, cols=slice(0, E)):
            nc.gpsimd.tensor_tensor(out=weight[t][:, cols], in0=wm_raw[t][:, cols], in1=scale[t][:, cols], op=MULT)

        def scale_c(t, parts, which=None):
            for part in which or range(parts):
                cols = block(part, E // parts)
                nc.vector.scalar_tensor_tensor(
                    out=in_fours(residual[t][:, cols]),
                    in0=by_e(c_ps[t % 2])[:, block(part, P // parts)],
                    scalar=ca_col[:, t : t + 1],
                    in1=in_fours(cb_row[:, cols]),
                    op0=MULT,
                    op1=MULT,
                )

        def subtract(t, engine, parts, which=None):
            for part in which or range(parts):
                cols = block(part, E // parts)
                engine.tensor_tensor(
                    out=residual[t][:, cols], in0=residual[t][:, cols], in1=tg_raw[t][:, cols], op=SUBTRACT
                )

        def weigh(t, engine, parts):
            for part in range(parts):
                cols = block(part, E // parts)
                engine.tensor_tensor(
                    out=m_rows[:, block(t, E)][:, cols], in0=residual[t][:, cols], in1=weight[t][:, cols], op=MULT
                )

        def turn_m(t, copy):
            turn(m_rows[:, block(t, E)], grad_ps[t % 3])
            turned(copy, m_e[t], grad_ps[t % 3])

        def grad_a(t):
            quantize(m_e_codes[t], m_e_scales[t], m_e[t], E5M2)
            product(grad_ps[t % 3], m_e_codes[t], m_e_scales[t], E5M2, b_e_codes, b_e_scales)

        db_ps = (turn_ps[0], c_ps[0], cb_ps, turn_ps[1])

        def grad_b(j):
            quantize(m_d_codes[j], m_d_scales[j], m_weave[:, block(j, E)], E5M2)
            product(db_ps[j], m_d_codes[j], m_d_scales[j], E5M2, a_d_codes, a_d_scales)

        def scatter(move, window, values, part):
            move(windows[window].indirect(part_of_list(part, 2)), values[:, block(part, N // 2)])

        def scatter_whole(window, values):
            vector_copy(windows[window].indirect(offsets[:]), values)

        def stage(values, source):
            for part in range(2):
                scalar_copy(values[:, block(part, N // 2)], source[:, block(part, N // 2)])

        def store(target, window):
            nc.sync.dma_start(out=target, in_=windows[window])

        for s in range(PACK):
            nc.tensor.transpose(cb_ps[:, block(s)], cb_col[:, s : s + 1].to_broadcast([P, P]), ident)
        scalar_copy(in_fours(cb_row), by_e(cb_ps))
        for t in range(1, PACK):
            nc.scalar.activation(out=scale[t], in_=cb_row, func=COPY, scale=ca_col[:, t : t + 1])

        def b_plane(s, copy):
            into = turn_ps[(0, 0, 1, 0)[s]]
            turn(b_got[s], into)
            turned(copy, b_turn[s], into)

        def quantize_b(s):
            quantize(b_i_codes[:, block(s)], b_i_scales[:, block(s)], b_turn[s], E4M3)

        def correlate_first(into, cols):
            product(into, a_i_codes[0], a_i_scales[0], E4M3, b_i_codes[:, cols], b_i_scales[:, cols])

        def pairs(x, u):
            return x.rearrange("p (q u v) -> p u q v", u=2, v=2)[:, u]

        def half(x, u):
            return x[:, block(u, E // 2)].rearrange("p (q v) -> p q v", v=2)

        def scale_first(u):
            nc.vector.scalar_tensor_tensor(
                out=half(residual[0], u),
                in0=c_ps[u][:, 0 : 2 * P].rearrange("p (v q) -> p q v", v=2),
                scalar=ca_col[:, 0:1],
                in1=pairs(cb_row, u),
                op0=MULT,
                op1=MULT,
            )

        def subtract_first(u):
            nc.vector.tensor_tensor(
                out=half(difference, u), in0=half(residual[0], u), in1=pairs(tg_raw[0], u), op=SUBTRACT
            )

        def weigh_first(u):
            nc.vector.tensor_tensor(
                out=pairs(m_rows[:, block(0, E)], u), in0=half(difference, u), in1=pairs(weight[0], u), op=MULT
            )

        gather(vector_copy, b_got[0], b_raw[0])
        b_plane(0, scalar_copy)
        quantize_b(0)
        gather(vector_copy, a_got[0], a_raw[0])
        turn(a_got[0], turn_ps[1])
        turned(scalar_copy, a_turn[0], turn_ps[1])
        quantize(a_i_codes[0], a_i_scales[0], a_turn[0], E4M3)
        for s in (1, 2):
            gather(vector_copy, b_got[s], b_raw[s])
            b_plane(s, scalar_copy)
            quantize_b(s)
            if s == 1:
                correlate_first(c_ps[0][:, 0 : 2 * P], slice(0, 2 * P))
                scale_first(0)
            else:
                correlate_first(c_ps[1][:, block(0)], block(2))
        gather(vector_copy, b_got[3], b_raw[3], SPLIT, N)
        gather(scalar_move, b_got[3], b_raw[3], 0, SPLIT)
        weave(scalar_copy, b_weave, b_planes, 0, 4)
        b_plane(3, scalar_copy)
        weave(vector_copy, b_weave, b_planes, 1, 2)
        weave(vector_copy, b_weave, b_planes, 1, 4)
        for part in (1, 0):
            cols = block(part, N // 2)
            quantize(b_e_codes[:, cols], b_e_scales[:, cols], b_weave[:, block(part, 2 * N)], E4M3)
        quantize_b(3)
        correlate_first(c_ps[1][:, block(1)], block(3))
        weight[0] = sb("weight0", E, F32, tag="b_weave")
        weight_on_vector(0)
        gather(scalar_move, a_got[1], a_raw[1])
        scale_first(1)
        turn_a(1, scalar_copy, cb_ps)
        difference = sb("difference", E, F32, tag="wm_raw0")
        for u in range(2):
            subtract_first(u)
        for u in range(2):
            weigh_first(u)
        a_i_codes[1] = sb("a_i_codes1", P, U32, tag="b_weave")
        correlate(1)
        weight[1] = sb("weight1", E, F32, tag="a_turn1")
        weight_on_gpsimd(1)
        gather(scalar_move, a_got[2], a_raw[2])
        turn_m(0, vector_copy)
        turn_a(2, scalar_copy, turn_ps[0])
        scale_c(1, 2, (0,))
        quantize(m_e_codes[0], m_e_scales[0], m_e[0], E5M2)
        first_ps = (grad_ps[0], turn_ps[1])
        for part in range(2):
            cols = block(part, N // 2)
            product(first_ps[part][:, cols], m_e_codes[0], m_e_scales[0], E5M2, b_e_codes[:, cols], b_e_scales[:, cols])
        scale_c(1, 2, (1,))
        subtract(1, nc.vector, 2)
        correlate(2)
        weigh(1, nc.vector, 2)
        for part in range(2):
            cols = block(part, N // 2)
            scalar_copy(da[0][:, cols], first_ps[part][:, cols])
        gather(vector_copy, a_got[3], a_raw[3])
        late_weights = sb("late_weights", EARLY + E, F32, tag="wm_raw1")
        weight[2], weight[3] = late_weights[:, EARLY:], late_weights[:, 0:E]
        weight_on_gpsimd(2)
        weight_on_gpsimd(3, slice(0, EARLY))
        for part in range(2):
            scatter(scalar_move, 0, da[0], part)
        store(da_rows[0], 0)
        after_a3 = sb("after_a3", E + E // 2, F32, tag="a_raw3")
        residual[2], m_e[1] = after_a3[:, 0:E], after_a3[:, E:].bitcast(BF16)
        turn_m(1, vector_copy)
        scale_c(2, 1)
        grad_a(1)
        turn_a(3, vector_copy, turn_ps[1])
        subtract(2, nc.vector, 1)
        correlate(3)
        weigh(2, nc.vector, 1)
        weight_on_gpsimd(3, slice(EARLY, E))
        weave(scalar_copy, a_weave, a_planes, 0, 8)
        weave(vector_copy, a_weave, a_planes, 1, 2)
        stage(da[1], grad_ps[1])
        turn_m(2, vector_copy)
        scale_c(3, 1)
        grad_a(2)
        weave(vector_copy, a_weave, a_planes, 1, 8, 3)
        subtract(3, nc.vector, 2)
        weigh(3, nc.vector, 2)
        for part in range(2):
            scatter(scalar_move, 1, da[1], part)
        store(da_rows[1], 1)
        weave(vector_copy, m_weave, m_planes, 0, 4)
        quantize(a_d_codes, a_d_scales, a_weave, E4M3)
        grad_b(0)
        stage(da[2], grad_ps[2])
        for part in range(2):
            scatter(scalar_move, 2, da[2], part)
        store(da_rows[2], 2)
        weave(vector_copy, m_weave, m_planes, 1, 4)
        turn_m(3, vector_copy)
        grad_b(1)
        weave(vector_copy, m_weave, m_planes, 2, 4)
        grad_a(3)
        vector_copy(db[0], db_ps[0])
        grad_b(2)
        scatter_whole(3, db[0])
        store(db_rows[0], 3)
        weave(vector_copy, m_weave, m_planes, 3, 4)
        stage(db[1], db_ps[1])
        vector_copy(da[3], grad_ps[0])
        grad_b(3)
        for part in range(2):
            scatter(scalar_move, 4, db[1], part)
        store(db_rows[1], 4)
        scatter_whole(0, da[3])
        store(da_rows[3], 0)
        stage(db[2], db_ps[2])
        vector_copy(db[3], db_ps[3])
        for part in range(2):
            scatter(scalar_move, 1, db[2], part)
        store(db_rows[2], 1)
        scatter_whole(2, db[3])
        store(db_rows[3], 2)
